import numpy as np, ml_dtypes
CORES = [3,11,19,27,35,43,51,59]
N = 8
import mx_ref
BF = ml_dtypes.bfloat16
def gentries(a):
    return np.ascontiguousarray(a.reshape(8, 16, -1).transpose(0, 2, 1)).reshape(8, -1)
def gtable(e):
    e = np.asarray(e); return np.ascontiguousarray(e.reshape(8, -1, 16).transpose(0, 2, 1)).reshape(128, -1).astype(np.int32)
def gcols(t, e):
    v = np.concatenate([t.reshape(8, 16, -1, 4), np.zeros((8, 16, 1, 4), BF)], axis=2)
    return np.ascontiguousarray(np.stack([v[g][:, e[g]] for g in range(8)])).reshape(128, -1)
def tile(rs):
    return np.stack(rs, axis=2).reshape(128, -1).astype(BF)
def cut(t, i, w=512):
    return t[:, w * i:w * i + w]
def pick(q, e):
    c = np.concatenate([q[0].reshape(128, -1, 4), np.zeros((128, 1, 4), np.uint8)], axis=1); s = np.concatenate([q[1], np.ones((16, 1), np.uint8)], axis=1)
    return (np.ascontiguousarray(c[:, e].reshape(128, -1)), np.ascontiguousarray(s[:, e]))
def join(*qs):
    return (np.concatenate([q[0] for q in qs], axis=1), np.concatenate([q[1] for q in qs], axis=1))
def put(q, e, v):
    c, s = q[0].reshape(128, -1, 4).copy(), q[1].copy(); c[:, e] = v[0].reshape(128, -1, 4); s[:, e] = v[1]
    return (c.reshape(128, -1), s)
def pk(c, s):
    return (np.ascontiguousarray(c), mx_ref.live(s))
def emit(q):
    return q[0], q[1]
def packed(v, rng):
    q = [mx_ref.quantize(np.ascontiguousarray(v[r])) for r in range(N)]
    return np.stack([a for a, b in q]), np.stack([mx_ref.plane(b, rng) for a, b in q])
def values_of_codes():
    e, c = np.zeros((128, 128, 4), np.float32), np.zeros((128, 2, 4), np.uint8)
    e[np.arange(128), np.arange(128), 0] = 1
    c[:127, :, 0] = np.arange(256).reshape(2, 128).T[:127]
    return mx_ref.matmul(mx_ref.quantize(e.reshape(128, 512).astype(BF)), (c.reshape(128, 8), np.full((16, 2), 127, np.uint8))).T.reshape(-1).astype(np.float64)
CODE_VALUE, SCALE_VALUE = values_of_codes(), 2.0 ** (np.arange(256) - 127.0)
def decode(q):
    return (CODE_VALUE[q[0]].reshape(16, 8, -1, 4) * SCALE_VALUE[q[1]][:, None, :, None] + 0.0).reshape(128, -1).astype(np.float32)
def f(rng, *shape):
    return mx_ref.flush((rng.standard_normal(shape, dtype=np.float32) * np.exp2(rng.integers(-2, 3, shape[:-1] + (1,)))).astype(BF))
def wide(rng, *shape, cols=0):
    v = rng.standard_normal(shape, dtype=np.float32) * np.exp2(rng.integers(-12, 13, shape)).astype(np.float32)
    if cols: v *= np.repeat(np.exp2(rng.integers(-cols, cols + 1, shape[:-2] + (1, shape[-1] // 4))) * (rng.random(shape[:-2] + (1, shape[-1] // 4)) > 0.0625), 4, axis=-1).astype(np.float32)
    return mx_ref.flush(v.astype(BF))
C, V, K, R = 320, 64, 96, 3
STEP = [1, 2, 4]
def big(v):
    v = v.astype(np.float32)
    v[np.abs(v) < np.float32(2.0 ** -16)] = 0
    return v.astype(BF)
def lists(a):
    return np.stack([gtable(a[r]) for r in range(N)])
def numbers_of(rng):
    return {"x": big(f(rng, N, 128, 4 * C)), "e": big(f(rng, N, 128, 16 * V)), "ex": lists(rng.integers(0, V, (N, 8, 4 * V))), "at": lists(rng.integers(0, V, (N, 8, C))), "u": np.array(f(rng, N, 128, 512)), "v": np.array(f(rng, N, 128, 512))}
def layers(rng):
    return big(f(rng, N, 128, 2048)).reshape(N, 8, 16, 4, 8, 16, 4)
def weights(rng, w):
    c, p = packed(np.ascontiguousarray(w).reshape(N, 128, 2048), rng)
    return {"wc": c, "ws": p}
def signs(rng):
    return np.stack([rng.permutation(8) % 2 * 2.0 - 1.0 for r in range(N)])
def setup_inputs(rng):
    return {**numbers_of(rng), **weights(rng, layers(rng))}
def setup_inputs_ties(rng):
    d = numbers_of(rng)
    o = rng.permutation(N)
    x, e = d["x"].reshape(N, 8, 16, C, 4), d["e"].reshape(N, 8, 16, 4 * V, 4)
    for r in range(N):
        k = np.zeros(C, int) if r == o[0] else rng.permutation(C) % 3
        a = x[r][:, :8, :3].copy()
        a[:, :, 2] = 0
        x[r][:, :8] = a[:, :, k]
        e[r][:, :8] = a[:, :, rng.permutation(4 * V) % 3]
    x[o[1]] = 0
    at = gentries(d["at"][o[1]]).copy()
    for g in rng.permutation(8)[:4]: at[g] = rng.integers(V)
    d["at"][o[1]] = gtable(at)
    u = d["u"].reshape(N, 8, 16, 128, 4)
    u[:, :, 8:, ::16] = 0
    d["x"], d["e"], d["u"] = x.reshape(N, 128, 4 * C), e.reshape(N, 128, 16 * V), u.reshape(N, 128, 512)
    w = layers(rng)
    w[:, :, 8:, :, :, :8] = 0
    return {**d, **weights(rng, w)}
def setup_inputs_near(rng):
    d = numbers_of(rng)
    m = C + 4 * V
    x = np.zeros((N, 8, 16, m, 4), np.float32)
    at = np.zeros((N, 8, C), int)
    u = d["u"].reshape(N, 128, 128, 4)
    u[:, :, ::16] = 0
    o, c = rng.permutation(N) % 4, signs(rng)
    x[:, :, 10:] = rng.integers(4, 8, (N, 8, 6, m, 4)) * 2.0 ** -20
    for r in range(N):
        if o[r] < 2:
            s = ((np.arange(m) + rng.integers(0, C, (8, 1))) % C + 1) // 2
            g = ((s[:, :, None] >> np.arange(8)) & 1) * np.exp2(np.arange(8) - 23.0)
            x[r, :, :2, :, 0] = c[r][:, None, None]
            x[r, :, 8] = g[:, :, :4]
            x[r, :, 9] = g[:, :, 4:]
            at[r] = np.argsort(rng.random((8, V)), axis=1)[:, np.arange(C) // 8]
        else:
            x[r, :, :2, :, 0] = rng.integers(8, 14, (8, 2, m)) * 2.0 ** -31
            at[r] = rng.integers(0, 4, (8, C))
        k = 1.0 if o[r] == 0 else 2.0 ** -30
        for h in range(0, 128, 16):
            u[r, h, h, 0] = k
            u[r, h + 8:h + 10, h] = k
            if o[r] >= 2:
                u[r, h, h, 0] = 9 * 2.0 ** -33
                u[r, h + 1, h, 0] = 8 * 2.0 ** -33
    x = x.astype(BF)
    d["x"], d["e"] = np.ascontiguousarray(x[:, :, :, :C]).reshape(N, 128, 4 * C), np.ascontiguousarray(x[:, :, :, C:]).reshape(N, 128, 16 * V)
    d["at"], d["u"] = lists(at), u.reshape(N, 128, 512)
    w = layers(rng)
    w[:, :, :10] = 0
    w[:, :, :, :, :, :10] = 0
    return {**d, **weights(rng, w)}
def setup_inputs_huge(rng):
    d = numbers_of(rng)
    m = C + 4 * V
    c = rng.integers(0, 2, (N, m)) * 2.0 - 1.0
    c[:, :C] = np.stack([rng.permutation(C) % 2 * 2.0 - 1.0 for r in range(N)])
    c[rng.permutation(N) < N // 2] = -1
    x = ((0.6 + 0.2 * rng.random((N, 128, m, 4))) * np.where(c < 0, -2.0 ** 30, 2.0 ** 28)[:, None, :, None]).astype(np.float32).astype(BF)
    d["x"], d["e"] = np.ascontiguousarray(x[:, :, :C]).reshape(N, 128, 4 * C), np.ascontiguousarray(x[:, :, C:]).reshape(N, 128, 16 * V)
    u = d["u"].reshape(N, 128, 128, 4)
    a = 2.0 ** 30 * (1 - 0.25 * rng.random((N, 128, 8, 4))) * signs(rng)[:, None, :, None]
    u[:, :, ::16] = a.astype(np.float32).astype(BF)
    d["u"] = u.reshape(N, 128, 512)
    w = np.zeros((N, 128, 4, 128, 4), np.float32)
    i = np.arange(128)
    for b in range(4): w[:, i, b, i, b] = 16
    return {**d, **weights(rng, w.astype(BF))}
def setup_inputs_crowd(rng):
    d = setup_inputs(rng)
    at, ex = rng.integers(0, V, (N, 8, C)), rng.integers(0, V, (N, 8, 4 * V))
    for r in range(N):
        for g, i in enumerate(rng.permutation(8)):
            a, b = rng.permutation(V)[:2]
            if i < 4:
                at[r, g] = np.where(rng.permutation(C) < C - i, a, b)
                ex[r, g, 4 * a:4 * a + 4] = a
                ex[r, g, 4 * b:4 * b + 4] = b
            if i == 4: ex[r, g] = a
            if i == 5:
                at[r, g] = rng.integers(K // 4, V, C)
                ex[r, g] = rng.integers(K // 4, V, 4 * V)
            if i == 6:
                at[r, g] = rng.integers(0, K // 4, C)
                ex[r, g] = rng.integers(0, K // 4, 4 * V)
            if i == 7:
                at[r, g] = rng.permutation(C) % V
                ex[r, g] = (np.arange(4 * V) // 4 + 1) % V
    d["ex"], d["at"] = lists(ex), lists(at)
    return d
def setup_inputs_spread(rng):
    d = setup_inputs(rng)
    d["x"], d["e"] = big(wide(rng, N, 128, 4 * C, cols=6)), big(wide(rng, N, 128, 16 * V, cols=6))
    return d
def check_inputs(d):
    b = []
    for k in ("x", "e", "u", "v"):
        a = np.abs(d[k].astype(np.float32))
        if not (np.isfinite(a).all() and ((a == 0) | (a >= 2.0 ** -30) & (a <= 2.0 ** 30)).all()): b.append("a value of " + k)
    for k in ("ex", "at"):
        if ((d[k] < 0) | (d[k] >= V)).any(): b.append("an entry of " + k)
    none, least, most = [emit(mx_ref.quantize(np.full((128, 16), k, np.float32).astype(BF)))[1][0, 0] for k in (0.0, 2.0 ** -30, 2.0 ** 30)]
    for r in range(N):
        if ((d["wc"][r] == 0x7F) | (d["wc"][r] == 0xFF)).any(): b.append("wc: a code that is no number")
        s = mx_ref.live(d["ws"][r])
        if ((s != none) & ((s < least) | (s > most))).any(): b.append("ws: a scale out of range")
    return b
def reference(x, e, ex, at, u, v, wc, ws):
    qu = [mx_ref.quantize(u[r]) for r in range(N)]
    lay = [pk(wc[r], ws[r]) for r in range(N)]
    now, mem = [x[r] for r in range(N)], [e[r] for r in range(N)]
    to, node = [gentries(ex[r]) for r in range(N)], [gentries(at[r]) for r in range(N)]
    rot = [np.zeros((8, V), np.int64) for r in range(N)]
    came_by = [None] * N
    num, group = np.arange(C), np.arange(8)[:, None]
    for t in range(R):
        sent = []
        for r in range(N):
            s = mx_ref.matmul(qu[r], mx_ref.quantize(now[r]))[::16] + np.float32(0.0)
            n, a, b = node[r], s[:, :, None], s[:, None, :]
            first = (n[:, :, None] == n[:, None, :]) & ((a > b) | (a == b) & (num[:, None] < num))
            k = np.sum(first, axis=1)
            way = 4 * n + (rot[r][group, n] + k) % 4
            o = np.lexsort((k, way))
            w = np.take_along_axis(way, o, axis=1)
            follows = np.zeros((8, C), bool)
            follows[:, 1:] = w[:, 1:] == w[:, :-1]
            pred = np.zeros((8, C), np.int64)
            np.put_along_axis(pred, o, np.where(follows, np.roll(o, 1, axis=1), C + w), axis=1)
            last = np.tile(C + np.arange(4 * V), (8, 1))
            g, i = np.nonzero(np.concatenate([~follows[:, 1:], np.ones((8, 1), bool)], axis=1))
            last[g, w[g, i]] = o[g, i]
            p = gcols(np.concatenate([now[r], mem[r]], axis=1), pred)
            z = ((now[r].astype(np.float32) + p.astype(np.float32)) * np.float32(0.5)).astype(BF)
            q = mx_ref.quantize(z)
            h = tile([np.maximum(mx_ref.matmul(pick(lay[r], np.arange(128 * b, 128 * b + 128)), q), np.float32(0.0)) * np.float32(0.03125) + z[:, b::4].astype(np.float32) for b in range(4)])
            mem[r] = gcols(np.concatenate([h, mem[r]], axis=1), last)
            rot[r] = (rot[r] + np.sum(n[:, :, None] == np.arange(V), axis=1)) % 4
            stack = np.lexsort((k, way, to[r][group, way]))
            now[r] = gcols(h, stack)
            came_by[r] = np.take_along_axis(way, stack, axis=1)
            node[r] = to[r][group, came_by[r]]
            sent.append(mx_ref.quantize(np.ascontiguousarray(cut(mem[r], 0, 4 * K))))
        came = decode(join(*sent)).astype(BF)
        for r in range(N): mem[r] = np.concatenate([cut(came, r ^ STEP[t], 4 * K), mem[r][:, 4 * K:]], axis=1)
    y, ot = np.zeros((N, 128, C), np.float32), np.zeros((N, 8, C), np.float32)
    oc, osc = np.zeros((N, 128, 16 * V), np.uint8), np.zeros((N, 16, 4 * V), np.uint8)
    for r in range(N):
        y[r] = mx_ref.matmul(mx_ref.quantize(v[r]), mx_ref.quantize(now[r]))
        ot[r] = came_by[r]
        oc[r], osc[r] = emit(mx_ref.quantize(np.ascontiguousarray(mem[r])))
    return {"y": y, "ot": ot, "oc": oc, "osc": osc}

@@ -1,0 +1,617 @@
+from concourse.mybir import dt, AluOpType, ActivationFunctionType
+
+ALU = AluOpType
+ACT = ActivationFunctionType
+C, V, KX, R = 320, 64, 96, 3
+NE = 4 * V
+STEP = [1, 2, 4]
+XB = [NE, NE + C, NE + 2 * C + KX, NE + 3 * C + 2 * KX]
+DB = [NE + 2 * C, NE + 3 * C + KX]
+NS = XB[3] + C
+TW = 1184
+KN = (2 * C + 1) * C
+BIG = float(2 ** 28)
+WHOLE = float(3 * 2 ** 22)
+ZA = 192
+TILES = [(0, 320), (320, 256), (576, 192), (768, 128), (896, 128)]
+MV2 = [2, 4, 4]
+PIECES = [(0, 24), (24, 52), (52, 80)]
+F8, U8, U16, I32, F32, B16 = "float8_e4m3fn_x4", "uint8", "uint16", "int32", "float32", "bfloat16"
+
+
+def _sb(n, d):
+    return ("sbuf", [128, n], d)
+
+
+SCRATCH = {
+    "st": _sb(4 * NS, B16), "xt": _sb(4 * 4 * C, B16), "et": _sb(4 * NE, B16), "ut": _sb(512, B16), "vt": _sb(512, B16),
+    "uq": _sb(128, F8), "us": _sb(128, U8), "up": _sb(128, F8), "ups": _sb(128, U8), "vq": _sb(128, F8), "vs": _sb(128, U8),
+    "wq": _sb(512, F8), "wp": _sb(512, U8), "xq": _sb(4 * C, F8), "xs": _sb(4 * C, U8), "zq": _sb(3 * C, F8), "zs": _sb(3 * C, U8),
+    "eb": _sb(2048, B16), "one": _sb(512, B16), "eq": _sb(512, F8), "es": _sb(512, U8), "zero": _sb(512, B16),
+    "zt": _sb(3 * 4 * C, B16), "zg": _sb(4 * C, B16), "rr": _sb(4 * C, F32), "mt": _sb(4 * NE, B16), "mq": _sb(NE, F8), "ms": _sb(NE, U8),
+    "xh": _sb(4 * C, B16), "bt": _sb(128 + 12 * KX, B16), "lq": _sb(128 + 3 * KX, F8), "ls": _sb(128 + 3 * KX, U8),
+    "yb": _sb(C, F32), "otb": _sb(C, F32),
+    "exi": _sb(16, I32), "ati": _sb(32, I32),
+    "iot": _sb(NS, F32), "t256": _sb(TW, F32), "t320": _sb(656, F32), "tn": _sb(64, F32),
+    "x16": _sb(C, B16), "x4": _sb(C, B16), "g8": _sb(512, B16), "ma": _sb(C, B16), "mb": _sb(C, B16), "m16": _sb(C, B16), "m4": _sb(C, B16),
+    "dm": _sb(C, B16), "k16": _sb(C, B16), "junk": _sb(8 * C, B16),
+    "sg": _sb(4096, B16), "sq": _sb(1024, F8), "sp": _sb(1024, U8), "bd": _sb(512, B16), "bdq": _sb(128, F8), "bds": _sb(128, U8),
+    "kp2": _sb(6 * C, B16), "cc": _sb(6 * C, B16), "cs": _sb(6 * C, B16),
+    "li": _sb(3072, I32), "lf": _sb(1280, F32), "lu": _sb(2048, U16), "rw": _sb(16384, F32), "rs": _sb(5632, F32),
+    "ps": ("psum", [128, 512 * 8], F32),
+}
+for _t in range(R):
+    SCRATCH["bq%d" % _t] = _sb(128, F8)
+    SCRATCH["bs%d" % _t] = _sb(128, U8)
+NDMA = 44
+SEMAPHORES = ["cv", "cs", "cp", "cg"] + ["d%d" % i for i in range(NDMA)] + ["arr%d" % t for t in range(R)] + ["snt%d" % t for t in range(R)]
+SIZE = {F8: 4, U8: 1, U16: 2, I32: 4, F32: 4, B16: 2}
+LOOK, TURNS, NOISE, SEED, KEPT, SOON, HEAT = 0.3, 5000, 8.0, 1, [], 0.2, 0.15
+CY, GA, SC, LAT = 0.83e-3 * 1.2, 1.5, 3.0, 0.08
+
+
+def W(name, lo, hi, step=1):
+    return (name, lo, hi, step, None)
+
+
+def IND(w, off):
+    return (w[0], w[1], w[2], 1, off)
+
+
+def sub(w, lo, hi, step=1):
+    return (w[0], w[1] + lo, w[1] + hi, step, None)
+
+
+def width(w):
+    return 16 * width(w[4]) if w[4] is not None else (w[2] - w[1] + w[3] - 1) // w[3]
+
+
+def meets(a, b):
+    if a[0] != b[0]:
+        return False
+    if a[0] == "ps":
+        return a[1] // 512 <= (b[2] - 1) // 512 and b[1] // 512 <= (a[2] - 1) // 512
+    if a[2] <= b[1] or b[2] <= a[1]:
+        return False
+    if a[3] == b[3] and a[3] > 1 and (a[1] - b[1]) % a[3] != 0:
+        return False
+    return True
+
+
+def plan(T, topo, core, rank):
+    ops = []
+    used = {"li": 0, "lf": 0, "lu": 0, "rw": 0, "rs": 0}
+    pool = ["rw"]
+
+    def new(buf, n):
+        a = used[buf]
+        used[buf] = a + (n + 7) // 8 * 8
+        return W(buf, a, a + n)
+
+    def ap(w, cast=None):
+        a = T[w[0]][:, w[1]:w[2]:w[3]] if w[3] > 1 else T[w[0]][:, w[1]:w[2]]
+        if cast is not None:
+            a = a.bitcast(cast)
+        if w[4] is not None:
+            a = a.indirect(ap(w[4]))
+        return a
+
+    def val(s):
+        return ap(s) if isinstance(s, tuple) else s
+
+    def add(eng, fn, reads, writes, cost, lat=0.0, kind="c"):
+        rd, wr = [], []
+        for w in reads:
+            if isinstance(w, tuple):
+                rd.append(w)
+                if w[4] is not None:
+                    rd.append(w[4])
+        for w in writes:
+            wr.append(w)
+            if w[4] is not None:
+                rd.append(w[4])
+        ops.append({"eng": eng, "fn": fn, "rd": rd, "wr": wr, "cost": cost, "lat": lat, "kind": kind})
+        return len(ops) - 1
+
+    def two(*ws):
+        return all(SIZE[SCRATCH[w[0]][2]] == 2 for w in ws)
+
+    def vcost(out, in0, f):
+        if out[4] is not None:
+            return 0.05 + SC * width(out) * CY
+        if in0[4] is not None:
+            return 0.05 + GA * width(in0) * CY
+        return 0.03 + max(40, f * width(out)) * CY
+
+    def ts(out, in0, s1, op0, s2=None, op1=None):
+        if op1 is None:
+            fn = lambda q: q.tensor_scalar(ap(out), ap(in0), val(s1), None, op0)
+        else:
+            fn = lambda q: q.tensor_scalar(ap(out), ap(in0), val(s1), val(s2), op0, op1)
+        add("v", fn, [in0, s1, s2], [out], vcost(out, in0, 0.5 if two(out, in0) else 1.0))
+        return out
+
+    def tt(out, in0, in1, op):
+        f = 1.0 if "ps" in (in0[0], in1[0]) else 2.0
+        add("v", lambda q: q.tensor_tensor(ap(out), ap(in0), ap(in1), op), [in0, in1], [out], vcost(out, in0, f))
+        return out
+
+    def cp(out, in_, cast=None):
+        add("v", lambda q: q.tensor_copy(ap(out, cast), ap(in_, cast)), [in_], [out], vcost(out, in_, 0.5 if two(out, in_) else 1.0))
+        return out
+
+    def scan(out, d0, d1, op0, op1):
+        add("v", lambda q: q.tensor_tensor_scan(ap(out), ap(d0), ap(d1), 0.0, op0, op1), [d0, d1], [out],
+            vcost(out, d0, 0.5 if two(out, d0, d1) else 1.0))
+        return out
+
+    def fill(out, c):
+        add("v", lambda q: q.memset(ap(out), c), [], [out], vcost(out, out, 0.5 if two(out) else 1.0))
+        return out
+
+    def act(out, in_, func, bias=None, scale=None, acc=None):
+        def fn(q):
+            kw = {}
+            if bias is not None:
+                kw["bias"] = val(bias)
+            if scale is not None:
+                kw["scale"] = val(scale)
+            if acc is not None:
+                kw["accum_out"] = ap(acc)
+            return q.activation(ap(out), ap(in_), func, **kw)
+        cost = 0.065 + GA * width(in_) * CY if in_[4] is not None else 0.04 + max(40, width(in_)) * CY
+        add("s", fn, [in_, bias, scale], [out] + ([acc] if acc is not None else []), cost + (0.02 if acc is not None else 0.0))
+        return out
+
+    def either(on_v, on_s):
+        on_v()
+        on_s()
+        o = ops.pop()
+        ops[-1]["alt"] = {"v": (ops[-1]["fn"], ops[-1]["cost"]), "s": (o["fn"], o["cost"])}
+
+    def aff(out, in_, scale=1.0):
+        either(lambda: ts(out, in_, scale, ALU.mult), lambda: act(out, in_, ACT.Copy, scale=scale))
+        return out
+
+    def relu(out, in_, scale):
+        either(lambda: ts(out, in_, 0.0, ALU.max, scale, ALU.mult), lambda: act(out, in_, ACT.Relu, scale=scale))
+        return out
+
+    def iota(out, pattern, base, cm):
+        if SCRATCH[out[0]][2] == I32:
+            fn = lambda q: q.iota(ap(out), pattern, base, cm)
+        else:
+            fn = lambda q: q.iota(ap(out), pattern, base, cm, allow_small_or_imprecise_dtypes=True)
+        add("g", fn, [], [out], 0.13 + 2 * width(out) * CY)
+        return out
+
+    def gfill(out, c):
+        return iota(out, [[0, width(out)]], c, 0)
+
+    def quant(q_, s_, in_):
+        add("v", lambda q: q.quantize_mx(ap(q_), ap(s_), ap(in_)), [in_], [q_, s_], 0.012 + 0.00022 * width(in_) * 1.2)
+
+    def mm(bank, a, as_, b, bs, start=True, stop=True):
+        out = W("ps", 512 * bank, 512 * bank + width(b))
+        add("p", lambda q: q.matmul_mx(ap(out), ap(a), ap(as_), ap(b), ap(bs), start, stop), [a, as_, b, bs], [out], (width(b) + 16) * 0.0007)
+        return out
+
+    def dma(eng, fn, reads, writes, lat):
+        add(eng, fn, reads, writes, 0.06, lat, "d")
+
+    def u16(in_, s1=None, op0=None, s2=None, op1=None):
+        o = new("lu", width(in_))
+        return cp(o, in_) if op0 is None else ts(o, in_, s1, op0, s2, op1)
+
+    def ti(in0, s1, op0, s2=None, op1=None):
+        return ts(new("li", width(in0)), in0, s1, op0, s2, op1)
+
+    def tf(in0, s1, op0, s2=None, op1=None):
+        return ts(new("lf", width(in0)), in0, s1, op0, s2, op1)
+
+    def tti(in0, in1, op):
+        return tt(new("li", width(in0)), in0, in1, op)
+
+    def ttf(in0, in1, op):
+        return tt(new("lf", width(in0)), in0, in1, op)
+
+    def rows(n):
+        return new(pool[0], n)
+
+    exi, ati = W("exi", 0, 16), W("ati", 0, 20)
+    xt = [W("xt", 4 * C * t, 4 * C * (t + 1)) for t in range(4)]
+    dma("y", lambda q: q.dma_start(ap(exi), T.ex[:]), [], [exi], 1.8)
+    dma("s", lambda q: q.dma_start(ap(ati), T.at[:]), [], [ati], 1.8)
+    dma("y", lambda q: q.dma_start(T.ut[:], T.u[:]), [], [W("ut", 0, 512)], 2.0)
+    dma("s", lambda q: q.dma_start(ap(xt[0]), T.x[:]), [], [xt[0]], 2.4)
+    dma("y", lambda q: q.dma_start(T.et[:], T.e[:]), [], [W("et", 0, 4 * NE)], 3.0)
+    dma("y", lambda q: q.dma_start(T.wq[:].bitcast(dt.uint8), T.wc[:]), [], [W("wq", 0, 512)], 3.5)
+    dma("y", lambda q: q.dma_start(T.wp[:], T.ws[:]), [], [W("wp", 0, 512)], 3.5)
+    dma("y", lambda q: q.dma_start(T.vt[:], T.v[:]), [], [W("vt", 0, 512)], 3.5)
+
+    pi = iota(new("li", 1), [[0, 1]], 0, 1)
+    io = W("iot", 0, NS)
+    for a, b in ((0, 336), (336, 896), (896, 1312), (1312, NS)):
+        iota(sub(io, a, b), [[1, b - a]], a, 0)
+    t256, t320, tn = W("t256", 0, TW), W("t320", 0, 656), W("tn", 0, 64)
+    for a, b in ((0, 80), (80, 640), (640, TW)):
+        iota(sub(t256, a, b), [[256, b - a]], 256 * a, 0)
+    iota(t320, [[C, 656]], 0, 0)
+    x16 = iota(W("x16", 0, C), [[0, 20], [1, 16]], 0, 0)
+    x4 = iota(W("x4", 0, C), [[0, 80], [1, 4]], 0, 0)
+    i16 = iota(new("li", 20), [[16, 20]], 0, 0)
+    ts(tn, sub(io, 0, 64), float(KN), ALU.mult)
+    ri = ti(pi, 15, ALU.bitwise_and)
+    qi = ti(ri, 2, ALU.arith_shift_right)
+    bi = ti(pi, 3, ALU.bitwise_and)
+    rf, qf, bf = cp(new("lf", 1), ri), cp(new("lf", 1), qi), cp(new("lf", 1), bi)
+    r1, q1 = tf(ri, 1.0, ALU.add), tf(qi, 1.0, ALU.add)
+    s16 = tf(ri, 15.0, ALU.is_equal, 1.0 / BIG, ALU.max)
+    s4 = tf(tf(qi, 3.0, ALU.is_equal, 1.0 / BIG, ALU.max), 4.0, ALU.mult)
+    bx = [tf(bi, -4.0 * XB[t], ALU.add) for t in range(R)]
+    cl = tf(i16, rf, ALU.add)
+    m16, m4, dm, k16 = W("m16", 0, C), W("m4", 0, C), W("dm", 0, C), W("k16", 0, C)
+    ma, mb = W("ma", 0, C), W("mb", 0, C)
+    ts(dm, x16, rf, ALU.is_equal, -1.0, ALU.mult)
+    ts(k16, x16, 1.0, ALU.min)
+    tt(m16, ts(ma, x16, rf, ALU.not_equal), ts(mb, x16, r1, ALU.is_equal, BIG, ALU.mult), ALU.max)
+    tt(m4, ts(ma, x4, qf, ALU.not_equal), ts(mb, x4, q1, ALU.is_equal, BIG, ALU.mult), ALU.max)
+    for a in range(0, 4096, 1024):
+        gfill(W("sg", a, a + 1024), 0)
+    gf = cp(new("lf", 1), ti(pi, 4, ALU.arith_shift_right))
+    g8 = iota(W("g8", 0, 512), [[1, 8], [0, 64]], 0, 0)
+    bdq, bds = W("bdq", 0, 128), W("bds", 0, 128)
+    quant(bdq, bds, ts(W("bd", 0, 512), g8, gf, ALU.is_equal, -float(C), ALU.mult))
+    kp2 = gfill(W("kp2", 0, max(MV2) * C), 1)
+    fill(W("kp2", 0, max(MV2) * C, C // 2), 0.0)
+    m15u = u16(i16, 15.0, ALU.add)
+    gfill(W("bt", 0, 128), 0)
+    quant(W("lq", 0, 128), W("ls", 0, 128), gfill(W("zero", 0, 512), 0))
+    one, eb = gfill(W("one", 0, 512), 1), W("eb", 0, 2048)
+    for b in range(4):
+        e_ = sub(eb, 512 * b, 512 * b + 512)
+        add("g", lambda q, b=b, e_=e_: q.affine_select(ap(e_), ap(one), [[-1, 512]], ALU.is_equal, 0.0, b, 4), [one], [e_], 0.17 + 1024 * CY)
+    quant(W("eq", 0, 512), W("es", 0, 512), eb)
+
+    def pick16(row):
+        n = width(row)
+        return sub(scan(rows(n), sub(m16, 0, n), row, ALU.mult, ALU.add), 15, n, 16)
+
+    def list4(row, col=None):
+        n = width(row)
+        return u16(sub(scan(rows(n), sub(m4, 0, n), row, ALU.mult, ALU.add), 3, n, 4), s4, ALU.mult, col or bf, ALU.add)
+
+    jn = [0]
+
+    def count_below(row, thr, more=0):
+        o = new("lf", width(thr) + more)
+        if more:
+            gfill(sub(o, width(thr), width(o)), width(row))
+        for m in range(width(thr)):
+            jn[0] = (jn[0] + 1) % 8
+            act(W("junk", C * jn[0], C * jn[0] + width(row)), row, ACT.Sign, bias=sub(thr, m, m + 1), scale=-1.0, acc=sub(o, m, m + 1))
+        return o
+
+    quant(W("uq", 0, 128), W("us", 0, 128), W("ut", 0, 512))
+    uu = u16(sub(i16, 0, 8))
+    up, ups = W("up", 0, 128), W("ups", 0, 128)
+    cp(up, IND(W("uq", 0, 128), uu), dt.uint32)
+    cp(ups, IND(W("us", 0, 128), uu))
+    quant(W("vq", 0, 128), W("vs", 0, 128), W("vt", 0, 512))
+    aff(W("st", 0, 4 * NE), W("et", 0, 4 * NE), 0.5)
+
+    def halve(t, a, b):
+        src, dst = aff(W("xh", a, b), sub(xt[t], a, b), 0.5), W("st", 4 * XB[t] + a, 4 * XB[t] + b)
+        dma("y", lambda q: q.dma_start(ap(dst), ap(src)), [src], [dst], 2.5)
+
+    halve(0, 0, 4 * C)
+
+    exu, atu = u16(exi), u16(ati)
+    kx = tt(rows(NE), IND(sub(t256, 0, 64), exu), sub(io, 0, NE), ALU.add)
+    kxl = ttf(tf(exi, 256.0, ALU.mult), sub(cl, 0, 16), ALU.add)
+    yu = u16(count_below(kx, kxl), 0.5, ALU.mult, (NE - 1) / 2.0, ALU.add)
+    ky = gfill(new("li", NE), 0)
+    cp(IND(ky, yu), kx)
+    ndrow = ti(ky, 8, ALU.arith_shift_right)
+    jrow = ti(ky, 255, ALU.bitwise_and)
+    jy = ti(pick16(jrow), s16, ALU.mult)
+    ns = ti(jy, 2, ALU.arith_shift_right)
+    nsu, nsu1 = u16(ns), u16(ns, 1.0, ALU.add)
+    uc = ti(ti(jy, 3, ALU.bitwise_and), -1.0, ALU.mult, 3.0, ALU.add)
+    c11 = ti(ns, 4.0, ALU.mult, 11.0, ALU.add)
+    cy = ti(sub(cl, 0, 16), float(C), ALU.add)
+    jm = tti(jy, ti(jy, float(KX), ALU.is_ge, 8192.0, ALU.mult), ALU.subtract)
+
+    def pair(tab, l1, l2):
+        a = aff(rows(NE), IND(tab, l1), 512.0)
+        pk = ti(pick16(tt(rows(NE), IND(tab, l2), a, ALU.add)), s16, ALU.mult)
+        return ti(pk, 9, ALU.arith_shift_right), ti(pk, 511, ALU.bitwise_and)
+
+    def as_row(lst, top):
+        return aff(rows(16 * width(lst)), IND(sub(io, 0, top), lst))
+
+    n4 = sub(cl, 0, 4)
+    ysu = u16(count_below(kx, tf(n4, 256.0, ALU.mult, -0.5, ALU.add), 1), 0.5, ALU.mult, NE / 2.0, ALU.add)
+    l1, l2 = pair(as_row(ysu, 336), nsu, nsu1)
+    l1u, l2u = u16(l1, 7.0, ALU.add), u16(l2, 7.0, ALU.add)
+
+    def node_keys(nl, nu):
+        base = tt(rows(C), IND(tn, nu), sub(io, 1, C + 1), ALU.add)
+        bl = ttf(tf(nl, float(KN), ALU.mult, C * C + 1 - WHOLE, ALU.add), cl, ALU.add)
+        return base, bl, tf(nl, 8.0, ALU.mult, float(16 + C - 1), ALU.add)
+
+    base, bl, pad = node_keys(ati, atu)
+    s0u = u16(count_below(base, tf(n4, float(KN), ALU.mult), 1), 0.5, ALU.mult, C / 2.0, ALU.add)
+    tab, la, lb = as_row(s0u, 336), nsu, nsu1
+    fo = gfill(new("li", 16), 0)
+    mp = jy
+    early = gfill(rows(TW + 8), 0)
+    tbl = sub(early, 8, TW + 8)
+    partner = [T.cores[rank ^ s] for s in STEP]
+
+    for t in range(R):
+        last = t == R - 1
+        sta, end = pair(tab, la, lb)
+        un = tti(tti(uc, end, ALU.add), sta, ALU.subtract)
+        slot = tti(tti(sta, c11, ALU.add), ti(uc, 3, ALU.bitwise_and), ALU.subtract)
+        slu = u16(slot, 2.0, ALU.mult)
+        fn_ = ti(un, 2, ALU.arith_shift_right)
+        ec = tti(fn_, fo, ALU.subtract)
+        ecrow = as_row(u16(ec), 336)
+        ee = rows(NE + 8)
+        gfill(sub(ee, 0, 8), 0)
+        scan(sub(ee, 8, NE + 8), ecrow, ecrow, ALU.add, ALU.max)
+        pe = pick16(sub(ee, 8, NE + 8))
+        eel = ti(pe, s16, ALU.mult)
+        big = ti(ec, 4096.0, ALU.mult)
+        offu = u16(tti(tti(cy, big, ALU.subtract), tti(eel, ec, ALU.subtract), ALU.max))
+        vrow = tt(rows(NE), IND(t256, slu), jrow if last else ndrow, ALU.add)
+        vw = gfill(rows(C + NE), 2048)
+        cp(IND(vw, offu), vrow)
+        keep = rows(C)
+        either(lambda keep=keep, vw=vw: ts(keep, sub(vw, 0, C), 2048.0, ALU.is_equal),
+               lambda keep=keep, vw=vw: act(keep, sub(vw, 0, C), ACT.Relu, bias=2049.0, scale=-1.0))
+        hv = ti(pick16(scan(rows(C), keep, sub(vw, 0, C), ALU.mult, ALU.add)), s16, ALU.mult)
+        fu = u16(ti(hv, 8, ALU.arith_shift_right))
+        code = ti(hv, 255, ALU.bitwise_and)
+        codeu = u16(code)
+        cp(IND(early, slu), as_row(u16(mp), 336 if t == 0 else DB[t - 1] + KX))
+        mpn = tti(tti(ti(pe, s16, ALU.mult, float(XB[t + 1] - 1), ALU.add), big, ALU.min), mp, ALU.max)
+        mrow = as_row(u16(mpn), XB[t + 1] + C)
+        nb = NE if last else KX
+        bu = list4(aff(rows(nb), IND(mrow, sub(yu, 0, nb // 16))))
+
+        pool[0], used["rs"] = "rs", 0
+        xq, xs = W("xq", C * t, C * t + C), W("xs", C * t, C * t + C)
+        quant(xq, xs, xt[t])
+        sv = mm(1, up, ups, xq, xs)
+        ss = mm(0, up, ups, xq, xs)
+        neg, ng = rows(C), rows(C)
+        for a, b in ((224, C), (0, 224)):
+            scan(sub(neg, a, b), sub(k16, a, b), tt(sub(ng, a, b), sub(sv, a, b), sub(dm, a, b), ALU.mult), ALU.mult, ALU.add)
+        ga = new("lf", 20)
+        gfill(sub(ga, 0, 1), 0)
+        pc = W("ps", 512 * 6, 512 * 6 + C)
+        for q_, (a, n_) in enumerate(TILES):
+            for k in range(4):
+                m = 20 - 4 * q_ - k
+                if m == 20:
+                    act(W("sg", 4 * a, 4 * (a + C), 4), tt(rows(C), sv, aff(rows(C), IND(neg, m15u)), ALU.add), ACT.Sign)
+                else:
+                    act(W("sg", 4 * a + k, 4 * (a + 16 * m), 4), sub(ss, 0, 16 * m), ACT.Sign, bias=sub(neg, 16 * m + 15, 16 * m + 16), acc=sub(ga, m, m + 1))
+            sq, sp = W("sq", a, a + n_), W("sp", a, a + n_)
+            quant(sq, sp, W("sg", 4 * a, 4 * (a + n_)))
+            mm(6, bdq, bds, sq, sp, q_ == 0, q_ == len(TILES) - 1)
+        key = tt(rows(C), pc, tt(rows(C), IND(t320, u16(ga, float(C), ALU.add)), base, ALU.add), ALU.add)
+        kl = ttf(tf(pick16(pc), s16, ALU.mult, WHOLE, ALU.add), ttf(tf(ga, float(C), ALU.mult), bl, ALU.add), ALU.add)
+        mv = MV2[t]
+        m0 = 20 - mv
+        pu = new("lu", 20)
+        cp(sub(pu, 0, m0), ttf(count_below(key, sub(kl, 0, m0)), sub(pad, 0, m0), ALU.add))
+        if mv:
+            for m in range(mv):
+                ts(W("cc", C * m, C * m + C), key, sub(kl, m0 + m, m0 + m + 1), ALU.is_lt, 2.0, ALU.mult)
+            scan(W("cs", 0, mv * C), sub(kp2, 0, mv * C), W("cc", 0, mv * C), ALU.mult, ALU.add)
+            both = ttf(W("cs", C // 2 - 1, mv * C, C), W("cs", C - 1, mv * C, C), ALU.add)
+            ts(sub(pu, m0, 20), ttf(both, sub(pad, m0, 20), ALU.add), float(1 - C), ALU.add)
+        cp(IND(tbl, pu), sub(io, XB[t], XB[t] + C))
+        zu = list4(aff(rows(C), IND(early, pu)))
+        su = list4(aff(rows(C), IND(tbl, fu)), bx[t])
+        top = XB[t] + C if t == 0 else DB[t - 1] + KX
+        zt = W("zt", 4 * C * t, 4 * C * (t + 1))
+        zq, zs = W("zq", C * t, C * t + C), W("zs", C * t, C * t + C)
+        f = 0.5 if last else 1.0
+        for h, (a, e_) in enumerate(((0, ZA), (ZA, C))):
+            tt(sub(zt, 4 * a, 4 * e_), IND(W("st", 0, 4 * top), sub(zu, a // 4, e_ // 4)), W("xh", 4 * a, 4 * e_), ALU.add)
+            quant(sub(zq, a, e_), sub(zs, a, e_), sub(zt, 4 * a, 4 * e_))
+            for b in range(4):
+                pr = mm((2 + 4 * h + b) % 8, W("wq", 128 * b, 128 * b + 128), W("wp", 128 * b, 128 * b + 128), sub(zq, a, e_), sub(zs, a, e_))
+                relu(W("rr", 4 * a + b, 4 * e_, 4), pr, 0.03125 * f)
+        for a, e_ in PIECES:
+            zg = aff(W("zg", 16 * a, 16 * e_), IND(zt, sub(su, a, e_)), f)
+            xh = W("st", 4 * XB[t + 1] + 16 * a, 4 * XB[t + 1] + 16 * e_)
+            tt(xh if last else sub(xt[t + 1], 16 * a, 16 * e_), IND(W("rr", 0, 4 * C), sub(su, a, e_)), zg, ALU.add)
+            if not last:
+                halve(t + 1, 16 * a, 16 * e_)
+        pool[0] = "rw"
+        win = W("st", 0, 4 * (XB[t + 1] + C))
+        bt, bq, bs = W("bt", 128 + 4 * KX * t, 128 + 4 * KX * (t + 1)), W("bq%d" % t, 0, 128), W("bs%d" % t, 0, 128)
+        if last:
+            aff(sub(bt, 0, 2 * KX), IND(win, sub(bu, 0, 12)), 2.0)
+            aff(sub(bt, 2 * KX, 4 * KX), IND(win, sub(bu, 12, 24)), 2.0)
+        else:
+            aff(bt, IND(win, sub(bu, 0, 24)), 2.0)
+        quant(bq, bs, sub(bt, -128, 4 * KX))
+        lq, ls = W("lq", 128 + KX * t, 128 + KX * (t + 1)), W("ls", 128 + KX * t, 128 + KX * (t + 1))
+        rid, pid, _ = topo.addr(partner[t])
+        mask = topo.mask(core, partner[t])
+        ne = len(topo.engines(core, partner[t]))
+
+        def send(src, dst, cast, t=t, rid=rid, pid=pid, mask=mask):
+            return lambda q: q.remote_dma(ap(dst, cast), ap(src, cast), T.sem["arr%d" % t], T.sem["snt%d" % t], pid, rid, mask)
+        i1 = add("g", send(sub(bq, 32, 128), lq, dt.uint8), [bq], [], 0.3, 0.0, "r")
+        i2 = add("g", send(sub(bs, 32, 128), ls, None), [bs], [], 0.3, 0.0, "r")
+        ia = add("x", None, [bq, bs], [lq, ls], 0.0, 2.0 if last else 6.0, "a")
+        ops[ia]["after"], ops[ia]["sem"], ops[ia]["n"] = [i1, i2], "arr%d" % t, 2 * ne
+        for b in range(4):
+            pd = mm(2 + b, W("eq", 128 * b, 128 * b + 128), W("es", 128 * b, 128 * b + 128), sub(lq, -32, KX), sub(ls, -32, KX))
+            if last:
+                aff(W("mt", b, 4 * KX, 4), sub(pd, 32, 128))
+            else:
+                aff(W("st", 4 * DB[t] + b, 4 * DB[t] + 4 * KX, 4), sub(pd, 32, 128), 0.5)
+        if not last:
+            mp = tti(ti(jm, float(DB[t]), ALU.add), mpn, ALU.max)
+            base, bl, pad = node_keys(code, codeu)
+            tab, la, lb, uc, fo = ee, l1u, l2u, un, fn_
+
+    otb = aff(W("otb", 0, C), IND(sub(io, 0, NE), codeu))
+    for gi in range(8):
+        dma("y", lambda q, gi=gi: q.dma_start(T.ot[gi:gi + 1, :], T.otb[16 * gi:16 * gi + 1, :]), [otb], [], 8.0)
+    xq, xs = W("xq", 3 * C, 4 * C), W("xs", 3 * C, 4 * C)
+    quant(xq, xs, aff(xt[3], W("st", 4 * XB[3], 4 * NS), 2.0))
+    yb = aff(W("yb", 0, C), mm(0, W("vq", 0, 128), W("vs", 0, 128), xq, xs))
+    dma("y", lambda q: q.dma_start(T.y[:], T.yb[:]), [yb], [], 2.2)
+    aff(W("mt", 4 * KX, 4 * NE), IND(win, sub(bu, 24, 64)), 2.0)
+    for a, queues in ((128, "yyyyy"), (0, "ysgys")):
+        mq, ms = W("mq", a, a + 128), W("ms", a, a + 128)
+        quant(mq, ms, W("mt", 4 * a, 4 * a + 512))
+        dma(queues[0], lambda q, a=a, mq=mq: q.dma_start(T.oc[:, 4 * a:4 * a + 512], ap(mq, dt.uint8)), [mq], [], 2.0)
+        for k in range(4):
+            dma(queues[1 + k], lambda q, a=a, k=k: q.dma_start(T.osc[4 * k:4 * k + 4, a:a + 128], T.ms[32 * k:32 * k + 4, a:a + 128]), [ms], [], 1.8)
+    return ops
+
+
+def order(ops):
+    n = len(ops)
+    seen = {}
+    for i, o in enumerate(ops):
+        dep = set(o.get("after", []))
+        for w in o["rd"]:
+            for j, x, wr in seen.get(w[0], []):
+                if (wr or (w[0] == "ps" and (ops[j]["eng"] != o["eng"] or "alt" in o or "alt" in ops[j]))) and meets(w, x):
+                    dep.add(j)
+        for w in o["wr"]:
+            for j, x, wr in seen.get(w[0], []):
+                if meets(w, x):
+                    dep.add(j)
+        dep.discard(i)
+        o["dep"] = dep
+        for w in o["rd"]:
+            seen.setdefault(w[0], []).append((i, w, False))
+        for w in o["wr"]:
+            seen.setdefault(w[0], []).append((i, w, True))
+    nxt = [[] for _ in range(n)]
+    for i, o in enumerate(ops):
+        for j in o["dep"]:
+            nxt[j].append(i)
+    prv = [sorted(o["dep"]) for o in ops]
+    lat = [o["lat"] for o in ops]
+
+    def run(before, after, pr, en, back):
+        cost = [o["alt"][en[i]][1] if "alt" in o else o["cost"] for i, o in enumerate(ops)]
+        left = [len(x) for x in before]
+        ready = {e: {} for e in "vspgyx"}
+        for i in range(n):
+            if left[i] == 0:
+                ready[en[i]][i] = lat[i] if back else 0.0
+        free, seq, t0, t1 = {e: 0.0 for e in ready}, [], [0.0] * n, [0.0] * n
+        for _ in range(n):
+            a, _p, e, i = min((max(r, free[e]), -pr[i], e, i) for e in ready for i, r in ready[e].items())
+            lim = a + LOOK * cost[i]
+            for j, r in ready[e].items():
+                if pr[j] > pr[i] and r < lim:
+                    i = j
+            a = max(ready[e].pop(i), free[e])
+            t0[i], free[e] = a, a + cost[i]
+            t1[i] = free[e] + (0.0 if back else lat[i])
+            seq.append(i)
+            for j in after[i]:
+                left[j] -= 1
+                if left[j] == 0:
+                    ready[en[j]][j] = max(t1[k] for k in before[j]) + LAT + (lat[j] if back else 0.0)
+        return seq, t0, t1
+
+    if not KEPT:
+        pr = [0.0] * n
+        for i in range(n - 1, -1, -1):
+            pr[i] = ops[i]["cost"] + lat[i] + LAT + max([pr[j] for j in nxt[i]] + [0.0])
+        free_ = [i for i in range(n) if "alt" in ops[i]]
+        en = ["s" if "alt" in o else o["eng"] for o in ops]
+        best, now, seed = None, None, [SEED]
+
+        def rnd():
+            seed[0] = (seed[0] * 1103515245 + 12345) % 2147483648
+            return seed[0] / 2147483648.0
+        for turn in range(TURNS):
+            if now is not None:
+                pr, en = list(now[5]), list(now[4])
+                move = rnd()
+                if move < 0.3:
+                    i = free_[int(rnd() * len(free_))]
+                    en[i] = "v" if en[i] == "s" else "s"
+                elif move < 0.93:
+                    a = int(rnd() * n)
+                    d = NOISE * (rnd() - 0.5) * rnd()
+                    for i in range(a, min(n, a + 1 + int(rnd() * rnd() * 40))):
+                        pr[i] += d
+                else:
+                    pr = run(nxt, prv, now[3], en, True)[2]
+            seq, t0, t1 = run(prv, nxt, pr, en, False)
+            mark = max(t1) + SOON * sum(t1) / n
+            if now is None or mark <= now[0] + HEAT * (1.0 - turn / TURNS) * rnd():
+                now = (mark, seq, t0, t1, en, pr)
+                if best is None or mark < best[0]:
+                    best = now
+        KEPT.append(best)
+    best = KEPT[0]
+    for i, o in enumerate(ops):
+        if "alt" in o:
+            o["eng"] = best[4][i]
+            o["fn"], o["cost"] = o["alt"][o["eng"]]
+        o["t0"], o["t1"] = best[2][i], best[3][i]
+    return best[1]
+
+
+def rank_program(g, core, T, topo):
+    rank = T.rank_of(core)
+    if rank is None:
+        return
+    ops = plan(T, topo, core, rank)
+    seq = order(ops)
+    queue = {"v": g.vector, "s": g.scalar, "p": g.tensor, "g": g, "y": g.sync}
+    counter = {"v": "cv", "s": "cs", "p": "cp", "g": "cg"}
+    count = {s: 0 for s in SEMAPHORES}
+    known = {e: {} for e in queue}
+    nd = 0
+    for i in seq:
+        o = ops[i]
+        if o["kind"] == "a":
+            o["mark"], o["clock"] = (o["sem"], o["n"]), {o["sem"]: o["n"]}
+            count[o["sem"]] = o["n"]
+            count["snt" + o["sem"][3:]] = o["n"]
+            continue
+        q, kn = queue[o["eng"]], known[o["eng"]]
+        for j in sorted(o["dep"], key=lambda j: -ops[j]["t1"]):
+            if ops[j]["kind"] == "r":
+                continue
+            s, c = ops[j]["mark"]
+            if kn.get(s, 0) < c:
+                q.wait_ge(T.sem[s], c)
+                for s2, c2 in ops[j]["clock"].items():
+                    kn[s2] = max(kn.get(s2, 0), c2)
+        ins = o["fn"](q)
+        if o["kind"] == "r":
+            continue
+        if o["kind"] == "d":
+            s, inc = "d%d" % nd, 16
+            nd += 1
+        else:
+            s, inc = counter[o["eng"]], 1
+        ins.then_inc(T.sem[s], inc)
+        count[s] += inc
+        o["mark"] = (s, count[s])
+        o["clock"] = dict(kn)
+        o["clock"][s] = count[s]
+    for s in SEMAPHORES:
+        if count[s]:
+            g.wait_ge(T.sem[s], count[s])

@@ -46,8 +46,8 @@ for _t in range(R):
 NDMA = 44
 SEMAPHORES = ["cv", "cs", "cp", "cg"] + ["d%d" % i for i in range(NDMA)] + ["arr%d" % t for t in range(R)] + ["snt%d" % t for t in range(R)]
 SIZE = {F8: 4, U8: 1, U16: 2, I32: 4, F32: 4, B16: 2}
-LOOK, TURNS, NOISE, SEED, KEPT, SOON, HEAT = 0.3, 5000, 8.0, 1, [], 0.2, 0.15
-CY, GA, SC, LAT = 0.83e-3 * 1.2, 1.5, 3.0, 0.08
+LOOK, TURNS, NOISE, SEED, KEPT, SOON, HEAT = 0.3, 9000, 8.0, 1, [], 0.5, 0.4
+PLANS = [(0.9e-3, 0.055, 20, 1.5, 3.4, 0.14), (1.0e-3, 0.03, 40, 1.5, 3.0, 0.08), (0.83e-3, 0.04, 40, 1.3, 3.0, 0.24)]
 
 
 def W(name, lo, hi, step=1):
@@ -78,7 +78,8 @@ def meets(a, b):
     return True
 
 
-def plan(T, topo, core, rank):
+def plan(T, topo, core, rank, model=0):
+    CY, FX, MN, GA, SC = PLANS[model][:5]
     ops = []
     used = {"li": 0, "lf": 0, "lu": 0, "rw": 0, "rs": 0}
     pool = ["rw"]
@@ -118,10 +119,10 @@ def plan(T, topo, core, rank):
 
     def vcost(out, in0, f):
         if out[4] is not None:
-            return 0.05 + SC * width(out) * CY
+            return FX + 0.02 + SC * width(out) * CY
         if in0[4] is not None:
-            return 0.05 + GA * width(in0) * CY
-        return 0.03 + max(40, f * width(out)) * CY
+            return FX + 0.02 + GA * width(in0) * CY
+        return FX + max(MN, f * width(out)) * CY
 
     def ts(out, in0, s1, op0, s2=None, op1=None):
         if op1 is None:
@@ -159,7 +160,7 @@ def plan(T, topo, core, rank):
             if acc is not None:
                 kw["accum_out"] = ap(acc)
             return q.activation(ap(out), ap(in_), func, **kw)
-        cost = 0.065 + GA * width(in_) * CY if in_[4] is not None else 0.04 + max(40, width(in_)) * CY
+        cost = FX + 0.035 + GA * width(in_) * CY if in_[4] is not None else FX + 0.01 + max(MN, width(in_)) * CY
         add("s", fn, [in_, bias, scale], [out] + ([acc] if acc is not None else []), cost + (0.02 if acc is not None else 0.0))
         return out
 
@@ -189,7 +190,7 @@ def plan(T, topo, core, rank):
         return iota(out, [[0, width(out)]], c, 0)
 
     def quant(q_, s_, in_):
-        add("v", lambda q: q.quantize_mx(ap(q_), ap(s_), ap(in_)), [in_], [q_, s_], 0.012 + 0.00022 * width(in_) * 1.2)
+        add("v", lambda q: q.quantize_mx(ap(q_), ap(s_), ap(in_)), [in_], [q_, s_], FX - 0.018 + 0.265 * width(in_) * CY)
 
     def mm(bank, a, as_, b, bs, start=True, stop=True):
         out = W("ps", 512 * bank, 512 * bank + width(b))
@@ -240,22 +241,24 @@ def plan(T, topo, core, rank):
     x16 = iota(W("x16", 0, C), [[0, 20], [1, 16]], 0, 0)
     x4 = iota(W("x4", 0, C), [[0, 80], [1, 4]], 0, 0)
     i16 = iota(new("li", 20), [[16, 20]], 0, 0)
-    ts(tn, sub(io, 0, 64), float(KN), ALU.mult)
+    aff(tn, sub(io, 0, 64), float(KN))
     ri = ti(pi, 15, ALU.bitwise_and)
     qi = ti(ri, 2, ALU.arith_shift_right)
     bi = ti(pi, 3, ALU.bitwise_and)
-    rf, qf, bf = cp(new("lf", 1), ri), cp(new("lf", 1), qi), cp(new("lf", 1), bi)
+    rf, qf, bf = aff(new("lf", 1), cp(new("lf", 1), ri)), cp(new("lf", 1), qi), cp(new("lf", 1), bi)
+    ops.pop(-3)
+    rf = ops[-3]["wr"][0]
     r1, q1 = tf(ri, 1.0, ALU.add), tf(qi, 1.0, ALU.add)
     s16 = tf(ri, 15.0, ALU.is_equal, 1.0 / BIG, ALU.max)
-    s4 = tf(tf(qi, 3.0, ALU.is_equal, 1.0 / BIG, ALU.max), 4.0, ALU.mult)
+    s4 = aff(new("lf", 1), tf(qi, 3.0, ALU.is_equal, 1.0 / BIG, ALU.max), 4.0)
     bx = [tf(bi, -4.0 * XB[t], ALU.add) for t in range(R)]
     cl = tf(i16, rf, ALU.add)
     m16, m4, dm, k16 = W("m16", 0, C), W("m4", 0, C), W("dm", 0, C), W("k16", 0, C)
     ma, mb = W("ma", 0, C), W("mb", 0, C)
     ts(dm, x16, rf, ALU.is_equal, -1.0, ALU.mult)
     ts(k16, x16, 1.0, ALU.min)
-    tt(m16, ts(ma, x16, rf, ALU.not_equal), ts(mb, x16, r1, ALU.is_equal, BIG, ALU.mult), ALU.max)
-    tt(m4, ts(ma, x4, qf, ALU.not_equal), ts(mb, x4, q1, ALU.is_equal, BIG, ALU.mult), ALU.max)
+    scan(m16, ts(ma, x16, rf, ALU.not_equal), ts(mb, x16, r1, ALU.is_equal, BIG, ALU.mult), ALU.min, ALU.max)
+    scan(m4, ts(ma, x4, qf, ALU.not_equal), ts(mb, x4, q1, ALU.is_equal, BIG, ALU.mult), ALU.min, ALU.max)
     for a in range(0, 4096, 1024):
         gfill(W("sg", a, a + 1024), 0)
     gf = cp(new("lf", 1), ti(pi, 4, ALU.arith_shift_right))
@@ -263,7 +266,7 @@ def plan(T, topo, core, rank):
     bdq, bds = W("bdq", 0, 128), W("bds", 0, 128)
     quant(bdq, bds, ts(W("bd", 0, 512), g8, gf, ALU.is_equal, -float(C), ALU.mult))
     kp2 = gfill(W("kp2", 0, max(MV2) * C), 1)
-    fill(W("kp2", 0, max(MV2) * C, C // 2), 0.0)
+    gfill(W("kp2", 0, max(MV2) * C, C // 2), 0)
     m15u = u16(i16, 15.0, ALU.add)
     gfill(W("bt", 0, 128), 0)
     quant(W("lq", 0, 128), W("ls", 0, 128), gfill(W("zero", 0, 512), 0))
@@ -296,7 +299,7 @@ def plan(T, topo, core, rank):
     uu = u16(sub(i16, 0, 8))
     up, ups = W("up", 0, 128), W("ups", 0, 128)
     cp(up, IND(W("uq", 0, 128), uu), dt.uint32)
-    cp(ups, IND(W("us", 0, 128), uu))
+    either(lambda: cp(ups, IND(W("us", 0, 128), uu)), lambda: act(ups, IND(W("us", 0, 128), uu), ACT.Copy))
     quant(W("vq", 0, 128), W("vs", 0, 128), W("vt", 0, 512))
     aff(W("st", 0, 4 * NE), W("et", 0, 4 * NE), 0.5)
 
@@ -323,7 +326,7 @@ def plan(T, topo, core, rank):
     jm = tti(jy, ti(jy, float(KX), ALU.is_ge, 8192.0, ALU.mult), ALU.subtract)
 
     def pair(tab, l1, l2):
-        a = aff(rows(NE), IND(tab, l1), 512.0)
+        a = aff(rows(NE), IND(tab, l1), 511.0)
         pk = ti(pick16(tt(rows(NE), IND(tab, l2), a, ALU.add)), s16, ALU.mult)
         return ti(pk, 9, ALU.arith_shift_right), ti(pk, 511, ALU.bitwise_and)
 
@@ -333,7 +336,7 @@ def plan(T, topo, core, rank):
     n4 = sub(cl, 0, 4)
     ysu = u16(count_below(kx, tf(n4, 256.0, ALU.mult, -0.5, ALU.add), 1), 0.5, ALU.mult, NE / 2.0, ALU.add)
     l1, l2 = pair(as_row(ysu, 336), nsu, nsu1)
-    l1u, l2u = u16(l1, 7.0, ALU.add), u16(l2, 7.0, ALU.add)
+    l1u, l2u = u16(l1, 7.0, ALU.add), u16(tti(l1, l2, ALU.add), 7.0, ALU.add)
 
     def node_keys(nl, nu):
         base = tt(rows(C), IND(tn, nu), sub(io, 1, C + 1), ALU.add)
@@ -343,7 +346,7 @@ def plan(T, topo, core, rank):
     base, bl, pad = node_keys(ati, atu)
     s0u = u16(count_below(base, tf(n4, float(KN), ALU.mult), 1), 0.5, ALU.mult, C / 2.0, ALU.add)
     tab, la, lb = as_row(s0u, 336), nsu, nsu1
-    fo = gfill(new("li", 16), 0)
+    fo = None
     mp = jy
     early = gfill(rows(TW + 8), 0)
     tbl = sub(early, 8, TW + 8)
@@ -351,12 +354,12 @@ def plan(T, topo, core, rank):
 
     for t in range(R):
         last = t == R - 1
-        sta, end = pair(tab, la, lb)
-        un = tti(tti(uc, end, ALU.add), sta, ALU.subtract)
-        slot = tti(tti(sta, c11, ALU.add), ti(uc, 3, ALU.bitwise_and), ALU.subtract)
+        sta, cnt = pair(tab, la, lb)
+        un = tti(uc, cnt, ALU.add)
+        slot = tti(tti(c11, ti(uc, 3, ALU.bitwise_and) if t else uc, ALU.subtract), sta, ALU.add)
         slu = u16(slot, 2.0, ALU.mult)
         fn_ = ti(un, 2, ALU.arith_shift_right)
-        ec = tti(fn_, fo, ALU.subtract)
+        ec = tti(fn_, fo, ALU.subtract) if t else fn_
         ecrow = as_row(u16(ec), 336)
         ee = rows(NE + 8)
         gfill(sub(ee, 0, 8), 0)
@@ -375,7 +378,7 @@ def plan(T, topo, core, rank):
         fu = u16(ti(hv, 8, ALU.arith_shift_right))
         code = ti(hv, 255, ALU.bitwise_and)
         codeu = u16(code)
-        cp(IND(early, slu), as_row(u16(mp), 336 if t == 0 else DB[t - 1] + KX))
+        cp(IND(early, slu), as_row(u16(mp), DB[t - 1] + KX) if t else jrow)
         mpn = tti(tti(ti(pe, s16, ALU.mult, float(XB[t + 1] - 1), ALU.add), big, ALU.min), mp, ALU.max)
         mrow = as_row(u16(mpn), XB[t + 1] + C)
         nb = NE if last else KX
@@ -470,18 +473,18 @@ def plan(T, topo, core, rank):
     xq, xs = W("xq", 3 * C, 4 * C), W("xs", 3 * C, 4 * C)
     quant(xq, xs, aff(xt[3], W("st", 4 * XB[3], 4 * NS), 2.0))
     yb = aff(W("yb", 0, C), mm(0, W("vq", 0, 128), W("vs", 0, 128), xq, xs))
-    dma("y", lambda q: q.dma_start(T.y[:], T.yb[:]), [yb], [], 2.2)
+    dma("y", lambda q: q.dma_start(T.y[:], T.yb[:]), [yb], [], 2.6)
     aff(W("mt", 4 * KX, 4 * NE), IND(win, sub(bu, 24, 64)), 2.0)
-    for a, queues in ((128, "yyyyy"), (0, "ysgys")):
+    for a, queues, lat in ((128, "yyyyy", 3.0), (0, "ysysy", 1.8)):
         mq, ms = W("mq", a, a + 128), W("ms", a, a + 128)
         quant(mq, ms, W("mt", 4 * a, 4 * a + 512))
-        dma(queues[0], lambda q, a=a, mq=mq: q.dma_start(T.oc[:, 4 * a:4 * a + 512], ap(mq, dt.uint8)), [mq], [], 2.0)
+        dma(queues[0], lambda q, a=a, mq=mq: q.dma_start(T.oc[:, 4 * a:4 * a + 512], ap(mq, dt.uint8)), [mq], [], lat + 0.2)
         for k in range(4):
-            dma(queues[1 + k], lambda q, a=a, k=k: q.dma_start(T.osc[4 * k:4 * k + 4, a:a + 128], T.ms[32 * k:32 * k + 4, a:a + 128]), [ms], [], 1.8)
+            dma(queues[1 + k], lambda q, a=a, k=k: q.dma_start(T.osc[4 * k:4 * k + 4, a:a + 128], T.ms[32 * k:32 * k + 4, a:a + 128]), [ms], [], lat)
     return ops
 
 
-def order(ops):
+def order(ops, others=()):
     n = len(ops)
     seen = {}
     for i, o in enumerate(ops):
@@ -506,6 +509,7 @@ def order(ops):
             nxt[j].append(i)
     prv = [sorted(o["dep"]) for o in ops]
     lat = [o["lat"] for o in ops]
+    wait = PLANS[0][5]
 
     def run(before, after, pr, en, back):
         cost = [o["alt"][en[i]][1] if "alt" in o else o["cost"] for i, o in enumerate(ops)]
@@ -528,13 +532,13 @@ def order(ops):
             for j in after[i]:
                 left[j] -= 1
                 if left[j] == 0:
-                    ready[en[j]][j] = max(t1[k] for k in before[j]) + LAT + (lat[j] if back else 0.0)
+                    ready[en[j]][j] = max(t1[k] for k in before[j]) + wait + (lat[j] if back else 0.0)
         return seq, t0, t1
 
     if not KEPT:
         pr = [0.0] * n
         for i in range(n - 1, -1, -1):
-            pr[i] = ops[i]["cost"] + lat[i] + LAT + max([pr[j] for j in nxt[i]] + [0.0])
+            pr[i] = ops[i]["cost"] + lat[i] + wait + max([pr[j] for j in nxt[i]] + [0.0])
         free_ = [i for i in range(n) if "alt" in ops[i]]
         en = ["s" if "alt" in o else o["eng"] for o in ops]
         best, now, seed = None, None, [SEED]
@@ -558,6 +562,17 @@ def order(ops):
                     pr = run(nxt, prv, now[3], en, True)[2]
             seq, t0, t1 = run(prv, nxt, pr, en, False)
             mark = max(t1) + SOON * sum(t1) / n
+            for k, other in enumerate(others):
+                wake, free, end = PLANS[k + 1][5], {e: 0.0 for e in "vspgyx"}, [0.0] * n
+                for i in seq:
+                    a = free[en[i]]
+                    for j in prv[i]:
+                        if end[j] > a:
+                            a = end[j]
+                    o = other[i]
+                    free[en[i]] = a = a + (o["alt"][en[i]][1] if "alt" in o else o["cost"])
+                    end[i] = a + lat[i] + wake
+                mark += max(end)
             if now is None or mark <= now[0] + HEAT * (1.0 - turn / TURNS) * rnd():
                 now = (mark, seq, t0, t1, en, pr)
                 if best is None or mark < best[0]:
@@ -577,7 +592,7 @@ def rank_program(g, core, T, topo):
     if rank is None:
         return
     ops = plan(T, topo, core, rank)
-    seq = order(ops)
+    seq = order(ops, [] if KEPT else [plan(T, topo, core, rank, k) for k in range(1, len(PLANS))])
     queue = {"v": g.vector, "s": g.scalar, "p": g.tensor, "g": g, "y": g.sync}
     counter = {"v": "cv", "s": "cs", "p": "cp", "g": "cg"}
     count = {s: 0 for s in SEMAPHORES}

from concourse.mybir import dt, AluOpType, ActivationFunctionType

ALU = AluOpType
ACT = ActivationFunctionType
C, V, KX, R = 320, 64, 96, 3
NE = 4 * V
STEP = [1, 2, 4]
XB = [NE, NE + C, NE + 2 * C + KX, NE + 3 * C + 2 * KX]
DB = [NE + 2 * C, NE + 3 * C + KX]
NS = XB[3] + C
TW = 1184
KN = (2 * C + 1) * C
BIG = float(2 ** 28)
WHOLE = float(3 * 2 ** 22)
ZA = 192
TILES = [(0, 320), (320, 256), (576, 192), (768, 128), (896, 128)]
MV2 = [2, 4, 4]
PIECES = [(0, 24), (24, 52), (52, 80)]
F8, U8, U16, I32, F32, B16 = "float8_e4m3fn_x4", "uint8", "uint16", "int32", "float32", "bfloat16"


def _sb(n, d):
    return ("sbuf", [128, n], d)


SCRATCH = {
    "st": _sb(4 * NS, B16), "xt": _sb(4 * 4 * C, B16), "et": _sb(4 * NE, B16), "ut": _sb(512, B16), "vt": _sb(512, B16),
    "uq": _sb(128, F8), "us": _sb(128, U8), "up": _sb(128, F8), "ups": _sb(128, U8), "vq": _sb(128, F8), "vs": _sb(128, U8),
    "wq": _sb(512, F8), "wp": _sb(512, U8), "xq": _sb(4 * C, F8), "xs": _sb(4 * C, U8), "zq": _sb(3 * C, F8), "zs": _sb(3 * C, U8),
    "eb": _sb(2048, B16), "one": _sb(512, B16), "eq": _sb(512, F8), "es": _sb(512, U8), "zero": _sb(512, B16),
    "zt": _sb(3 * 4 * C, B16), "zg": _sb(4 * C, B16), "rr": _sb(4 * C, F32), "mt": _sb(4 * NE, B16), "mq": _sb(NE, F8), "ms": _sb(NE, U8),
    "xh": _sb(4 * C, B16), "bt": _sb(128 + 12 * KX, B16), "lq": _sb(128 + 3 * KX, F8), "ls": _sb(128 + 3 * KX, U8),
    "yb": _sb(C, F32), "otb": _sb(C, F32),
    "exi": _sb(16, I32), "ati": _sb(32, I32),
    "iot": _sb(NS, F32), "t256": _sb(TW, F32), "t320": _sb(656, F32), "tn": _sb(64, F32),
    "x16": _sb(C, B16), "x4": _sb(C, B16), "g8": _sb(512, B16), "ma": _sb(C, B16), "mb": _sb(C, B16), "m16": _sb(C, B16), "m4": _sb(C, B16),
    "dm": _sb(C, B16), "k16": _sb(C, B16), "junk": _sb(8 * C, B16),
    "sg": _sb(4096, B16), "sq": _sb(1024, F8), "sp": _sb(1024, U8), "bd": _sb(512, B16), "bdq": _sb(128, F8), "bds": _sb(128, U8),
    "kp2": _sb(6 * C, B16), "cc": _sb(6 * C, B16), "cs": _sb(6 * C, B16),
    "li": _sb(3072, I32), "lf": _sb(1280, F32), "lu": _sb(2048, U16), "rw": _sb(16384, F32), "rs": _sb(5632, F32),
    "ps": ("psum", [128, 512 * 8], F32),
}
for _t in range(R):
    SCRATCH["bq%d" % _t] = _sb(128, F8)
    SCRATCH["bs%d" % _t] = _sb(128, U8)
NDMA = 44
SEMAPHORES = ["cv", "cs", "cp", "cg"] + ["d%d" % i for i in range(NDMA)] + ["arr%d" % t for t in range(R)] + ["snt%d" % t for t in range(R)]
SIZE = {F8: 4, U8: 1, U16: 2, I32: 4, F32: 4, B16: 2}
LOOK, TURNS, NOISE, SEED, KEPT, SOON, HEAT = 0.3, 9000, 8.0, 1, [], 0.5, 0.4
PLANS = [(0.9e-3, 0.055, 20, 1.5, 3.4, 0.14), (1.0e-3, 0.03, 40, 1.5, 3.0, 0.08), (0.83e-3, 0.04, 40, 1.3, 3.0, 0.24)]


def W(name, lo, hi, step=1):
    return (name, lo, hi, step, None)


def IND(w, off):
    return (w[0], w[1], w[2], 1, off)


def sub(w, lo, hi, step=1):
    return (w[0], w[1] + lo, w[1] + hi, step, None)


def width(w):
    return 16 * width(w[4]) if w[4] is not None else (w[2] - w[1] + w[3] - 1) // w[3]


def meets(a, b):
    if a[0] != b[0]:
        return False
    if a[0] == "ps":
        return a[1] // 512 <= (b[2] - 1) // 512 and b[1] // 512 <= (a[2] - 1) // 512
    if a[2] <= b[1] or b[2] <= a[1]:
        return False
    if a[3] == b[3] and a[3] > 1 and (a[1] - b[1]) % a[3] != 0:
        return False
    return True


def plan(T, topo, core, rank, model=0):
    CY, FX, MN, GA, SC = PLANS[model][:5]
    ops = []
    used = {"li": 0, "lf": 0, "lu": 0, "rw": 0, "rs": 0}
    pool = ["rw"]

    def new(buf, n):
        a = used[buf]
        used[buf] = a + (n + 7) // 8 * 8
        return W(buf, a, a + n)

    def ap(w, cast=None):
        a = T[w[0]][:, w[1]:w[2]:w[3]] if w[3] > 1 else T[w[0]][:, w[1]:w[2]]
        if cast is not None:
            a = a.bitcast(cast)
        if w[4] is not None:
            a = a.indirect(ap(w[4]))
        return a

    def val(s):
        return ap(s) if isinstance(s, tuple) else s

    def add(eng, fn, reads, writes, cost, lat=0.0, kind="c"):
        rd, wr = [], []
        for w in reads:
            if isinstance(w, tuple):
                rd.append(w)
                if w[4] is not None:
                    rd.append(w[4])
        for w in writes:
            wr.append(w)
            if w[4] is not None:
                rd.append(w[4])
        ops.append({"eng": eng, "fn": fn, "rd": rd, "wr": wr, "cost": cost, "lat": lat, "kind": kind})
        return len(ops) - 1

    def two(*ws):
        return all(SIZE[SCRATCH[w[0]][2]] == 2 for w in ws)

    def vcost(out, in0, f):
        if out[4] is not None:
            return FX + 0.02 + SC * width(out) * CY
        if in0[4] is not None:
            return FX + 0.02 + GA * width(in0) * CY
        return FX + max(MN, f * width(out)) * CY

    def ts(out, in0, s1, op0, s2=None, op1=None):
        if op1 is None:
            fn = lambda q: q.tensor_scalar(ap(out), ap(in0), val(s1), None, op0)
        else:
            fn = lambda q: q.tensor_scalar(ap(out), ap(in0), val(s1), val(s2), op0, op1)
        add("v", fn, [in0, s1, s2], [out], vcost(out, in0, 0.5 if two(out, in0) else 1.0))
        return out

    def tt(out, in0, in1, op):
        f = 1.0 if "ps" in (in0[0], in1[0]) else 2.0
        add("v", lambda q: q.tensor_tensor(ap(out), ap(in0), ap(in1), op), [in0, in1], [out], vcost(out, in0, f))
        return out

    def cp(out, in_, cast=None):
        add("v", lambda q: q.tensor_copy(ap(out, cast), ap(in_, cast)), [in_], [out], vcost(out, in_, 0.5 if two(out, in_) else 1.0))
        return out

    def scan(out, d0, d1, op0, op1):
        add("v", lambda q: q.tensor_tensor_scan(ap(out), ap(d0), ap(d1), 0.0, op0, op1), [d0, d1], [out],
            vcost(out, d0, 0.5 if two(out, d0, d1) else 1.0))
        return out

    def fill(out, c):
        add("v", lambda q: q.memset(ap(out), c), [], [out], vcost(out, out, 0.5 if two(out) else 1.0))
        return out

    def act(out, in_, func, bias=None, scale=None, acc=None):
        def fn(q):
            kw = {}
            if bias is not None:
                kw["bias"] = val(bias)
            if scale is not None:
                kw["scale"] = val(scale)
            if acc is not None:
                kw["accum_out"] = ap(acc)
            return q.activation(ap(out), ap(in_), func, **kw)
        cost = FX + 0.035 + GA * width(in_) * CY if in_[4] is not None else FX + 0.01 + max(MN, width(in_)) * CY
        add("s", fn, [in_, bias, scale], [out] + ([acc] if acc is not None else []), cost + (0.02 if acc is not None else 0.0))
        return out

    def either(on_v, on_s):
        on_v()
        on_s()
        o = ops.pop()
        ops[-1]["alt"] = {"v": (ops[-1]["fn"], ops[-1]["cost"]), "s": (o["fn"], o["cost"])}

    def aff(out, in_, scale=1.0):
        either(lambda: ts(out, in_, scale, ALU.mult), lambda: act(out, in_, ACT.Copy, scale=scale))
        return out

    def relu(out, in_, scale):
        either(lambda: ts(out, in_, 0.0, ALU.max, scale, ALU.mult), lambda: act(out, in_, ACT.Relu, scale=scale))
        return out

    def iota(out, pattern, base, cm):
        if SCRATCH[out[0]][2] == I32:
            fn = lambda q: q.iota(ap(out), pattern, base, cm)
        else:
            fn = lambda q: q.iota(ap(out), pattern, base, cm, allow_small_or_imprecise_dtypes=True)
        add("g", fn, [], [out], 0.13 + 2 * width(out) * CY)
        return out

    def gfill(out, c):
        return iota(out, [[0, width(out)]], c, 0)

    def quant(q_, s_, in_):
        add("v", lambda q: q.quantize_mx(ap(q_), ap(s_), ap(in_)), [in_], [q_, s_], FX - 0.018 + 0.265 * width(in_) * CY)

    def mm(bank, a, as_, b, bs, start=True, stop=True):
        out = W("ps", 512 * bank, 512 * bank + width(b))
        add("p", lambda q: q.matmul_mx(ap(out), ap(a), ap(as_), ap(b), ap(bs), start, stop), [a, as_, b, bs], [out], (width(b) + 16) * 0.0007)
        return out

    def dma(eng, fn, reads, writes, lat):
        add(eng, fn, reads, writes, 0.06, lat, "d")

    def u16(in_, s1=None, op0=None, s2=None, op1=None):
        o = new("lu", width(in_))
        return cp(o, in_) if op0 is None else ts(o, in_, s1, op0, s2, op1)

    def ti(in0, s1, op0, s2=None, op1=None):
        return ts(new("li", width(in0)), in0, s1, op0, s2, op1)

    def tf(in0, s1, op0, s2=None, op1=None):
        return ts(new("lf", width(in0)), in0, s1, op0, s2, op1)

    def tti(in0, in1, op):
        return tt(new("li", width(in0)), in0, in1, op)

    def ttf(in0, in1, op):
        return tt(new("lf", width(in0)), in0, in1, op)

    def rows(n):
        return new(pool[0], n)

    exi, ati = W("exi", 0, 16), W("ati", 0, 20)
    xt = [W("xt", 4 * C * t, 4 * C * (t + 1)) for t in range(4)]
    dma("y", lambda q: q.dma_start(ap(exi), T.ex[:]), [], [exi], 1.8)
    dma("s", lambda q: q.dma_start(ap(ati), T.at[:]), [], [ati], 1.8)
    dma("y", lambda q: q.dma_start(T.ut[:], T.u[:]), [], [W("ut", 0, 512)], 2.0)
    dma("s", lambda q: q.dma_start(ap(xt[0]), T.x[:]), [], [xt[0]], 2.4)
    dma("y", lambda q: q.dma_start(T.et[:], T.e[:]), [], [W("et", 0, 4 * NE)], 3.0)
    dma("y", lambda q: q.dma_start(T.wq[:].bitcast(dt.uint8), T.wc[:]), [], [W("wq", 0, 512)], 3.5)
    dma("y", lambda q: q.dma_start(T.wp[:], T.ws[:]), [], [W("wp", 0, 512)], 3.5)
    dma("y", lambda q: q.dma_start(T.vt[:], T.v[:]), [], [W("vt", 0, 512)], 3.5)

    pi = iota(new("li", 1), [[0, 1]], 0, 1)
    io = W("iot", 0, NS)
    for a, b in ((0, 336), (336, 896), (896, 1312), (1312, NS)):
        iota(sub(io, a, b), [[1, b - a]], a, 0)
    t256, t320, tn = W("t256", 0, TW), W("t320", 0, 656), W("tn", 0, 64)
    for a, b in ((0, 80), (80, 640), (640, TW)):
        iota(sub(t256, a, b), [[256, b - a]], 256 * a, 0)
    iota(t320, [[C, 656]], 0, 0)
    x16 = iota(W("x16", 0, C), [[0, 20], [1, 16]], 0, 0)
    x4 = iota(W("x4", 0, C), [[0, 80], [1, 4]], 0, 0)
    i16 = iota(new("li", 20), [[16, 20]], 0, 0)
    aff(tn, sub(io, 0, 64), float(KN))
    ri = ti(pi, 15, ALU.bitwise_and)
    qi = ti(ri, 2, ALU.arith_shift_right)
    bi = ti(pi, 3, ALU.bitwise_and)
    rf, qf, bf = aff(new("lf", 1), cp(new("lf", 1), ri)), cp(new("lf", 1), qi), cp(new("lf", 1), bi)
    ops.pop(-3)
    rf = ops[-3]["wr"][0]
    r1, q1 = tf(ri, 1.0, ALU.add), tf(qi, 1.0, ALU.add)
    s16 = tf(ri, 15.0, ALU.is_equal, 1.0 / BIG, ALU.max)
    s4 = aff(new("lf", 1), tf(qi, 3.0, ALU.is_equal, 1.0 / BIG, ALU.max), 4.0)
    bx = [tf(bi, -4.0 * XB[t], ALU.add) for t in range(R)]
    cl = tf(i16, rf, ALU.add)
    m16, m4, dm, k16 = W("m16", 0, C), W("m4", 0, C), W("dm", 0, C), W("k16", 0, C)
    ma, mb = W("ma", 0, C), W("mb", 0, C)
    ts(dm, x16, rf, ALU.is_equal, -1.0, ALU.mult)
    ts(k16, x16, 1.0, ALU.min)
    scan(m16, ts(ma, x16, rf, ALU.not_equal), ts(mb, x16, r1, ALU.is_equal, BIG, ALU.mult), ALU.min, ALU.max)
    scan(m4, ts(ma, x4, qf, ALU.not_equal), ts(mb, x4, q1, ALU.is_equal, BIG, ALU.mult), ALU.min, ALU.max)
    for a in range(0, 4096, 1024):
        gfill(W("sg", a, a + 1024), 0)
    gf = cp(new("lf", 1), ti(pi, 4, ALU.arith_shift_right))
    g8 = iota(W("g8", 0, 512), [[1, 8], [0, 64]], 0, 0)
    bdq, bds = W("bdq", 0, 128), W("bds", 0, 128)
    quant(bdq, bds, ts(W("bd", 0, 512), g8, gf, ALU.is_equal, -float(C), ALU.mult))
    kp2 = gfill(W("kp2", 0, max(MV2) * C), 1)
    gfill(W("kp2", 0, max(MV2) * C, C // 2), 0)
    m15u = u16(i16, 15.0, ALU.add)
    gfill(W("bt", 0, 128), 0)
    quant(W("lq", 0, 128), W("ls", 0, 128), gfill(W("zero", 0, 512), 0))
    one, eb = gfill(W("one", 0, 512), 1), W("eb", 0, 2048)
    for b in range(4):
        e_ = sub(eb, 512 * b, 512 * b + 512)
        add("g", lambda q, b=b, e_=e_: q.affine_select(ap(e_), ap(one), [[-1, 512]], ALU.is_equal, 0.0, b, 4), [one], [e_], 0.17 + 1024 * CY)
    quant(W("eq", 0, 512), W("es", 0, 512), eb)

    def pick16(row):
        n = width(row)
        return sub(scan(rows(n), sub(m16, 0, n), row, ALU.mult, ALU.add), 15, n, 16)

    def list4(row, col=None):
        n = width(row)
        return u16(sub(scan(rows(n), sub(m4, 0, n), row, ALU.mult, ALU.add), 3, n, 4), s4, ALU.mult, col or bf, ALU.add)

    jn = [0]

    def count_below(row, thr, more=0):
        o = new("lf", width(thr) + more)
        if more:
            gfill(sub(o, width(thr), width(o)), width(row))
        for m in range(width(thr)):
            jn[0] = (jn[0] + 1) % 8
            act(W("junk", C * jn[0], C * jn[0] + width(row)), row, ACT.Sign, bias=sub(thr, m, m + 1), scale=-1.0, acc=sub(o, m, m + 1))
        return o

    quant(W("uq", 0, 128), W("us", 0, 128), W("ut", 0, 512))
    uu = u16(sub(i16, 0, 8))
    up, ups = W("up", 0, 128), W("ups", 0, 128)
    cp(up, IND(W("uq", 0, 128), uu), dt.uint32)
    either(lambda: cp(ups, IND(W("us", 0, 128), uu)), lambda: act(ups, IND(W("us", 0, 128), uu), ACT.Copy))
    quant(W("vq", 0, 128), W("vs", 0, 128), W("vt", 0, 512))
    aff(W("st", 0, 4 * NE), W("et", 0, 4 * NE), 0.5)

    def halve(t, a, b):
        src, dst = aff(W("xh", a, b), sub(xt[t], a, b), 0.5), W("st", 4 * XB[t] + a, 4 * XB[t] + b)
        dma("y", lambda q: q.dma_start(ap(dst), ap(src)), [src], [dst], 2.5)

    halve(0, 0, 4 * C)

    exu, atu = u16(exi), u16(ati)
    kx = tt(rows(NE), IND(sub(t256, 0, 64), exu), sub(io, 0, NE), ALU.add)
    kxl = ttf(tf(exi, 256.0, ALU.mult), sub(cl, 0, 16), ALU.add)
    yu = u16(count_below(kx, kxl), 0.5, ALU.mult, (NE - 1) / 2.0, ALU.add)
    ky = gfill(new("li", NE), 0)
    cp(IND(ky, yu), kx)
    ndrow = ti(ky, 8, ALU.arith_shift_right)
    jrow = ti(ky, 255, ALU.bitwise_and)
    jy = ti(pick16(jrow), s16, ALU.mult)
    ns = ti(jy, 2, ALU.arith_shift_right)
    nsu, nsu1 = u16(ns), u16(ns, 1.0, ALU.add)
    uc = ti(ti(jy, 3, ALU.bitwise_and), -1.0, ALU.mult, 3.0, ALU.add)
    c11 = ti(ns, 4.0, ALU.mult, 11.0, ALU.add)
    cy = ti(sub(cl, 0, 16), float(C), ALU.add)
    jm = tti(jy, ti(jy, float(KX), ALU.is_ge, 8192.0, ALU.mult), ALU.subtract)

    def pair(tab, l1, l2):
        a = aff(rows(NE), IND(tab, l1), 511.0)
        pk = ti(pick16(tt(rows(NE), IND(tab, l2), a, ALU.add)), s16, ALU.mult)
        return ti(pk, 9, ALU.arith_shift_right), ti(pk, 511, ALU.bitwise_and)

    def as_row(lst, top):
        return aff(rows(16 * width(lst)), IND(sub(io, 0, top), lst))

    n4 = sub(cl, 0, 4)
    ysu = u16(count_below(kx, tf(n4, 256.0, ALU.mult, -0.5, ALU.add), 1), 0.5, ALU.mult, NE / 2.0, ALU.add)
    l1, l2 = pair(as_row(ysu, 336), nsu, nsu1)
    l1u, l2u = u16(l1, 7.0, ALU.add), u16(tti(l1, l2, ALU.add), 7.0, ALU.add)

    def node_keys(nl, nu):
        base = tt(rows(C), IND(tn, nu), sub(io, 1, C + 1), ALU.add)
        bl = ttf(tf(nl, float(KN), ALU.mult, C * C + 1 - WHOLE, ALU.add), cl, ALU.add)
        return base, bl, tf(nl, 8.0, ALU.mult, float(16 + C - 1), ALU.add)

    base, bl, pad = node_keys(ati, atu)
    s0u = u16(count_below(base, tf(n4, float(KN), ALU.mult), 1), 0.5, ALU.mult, C / 2.0, ALU.add)
    tab, la, lb = as_row(s0u, 336), nsu, nsu1
    fo = None
    mp = jy
    early = gfill(rows(TW + 8), 0)
    tbl = sub(early, 8, TW + 8)
    partner = [T.cores[rank ^ s] for s in STEP]

    for t in range(R):
        last = t == R - 1
        sta, cnt = pair(tab, la, lb)
        un = tti(uc, cnt, ALU.add)
        slot = tti(tti(c11, ti(uc, 3, ALU.bitwise_and) if t else uc, ALU.subtract), sta, ALU.add)
        slu = u16(slot, 2.0, ALU.mult)
        fn_ = ti(un, 2, ALU.arith_shift_right)
        ec = tti(fn_, fo, ALU.subtract) if t else fn_
        ecrow = as_row(u16(ec), 336)
        ee = rows(NE + 8)
        gfill(sub(ee, 0, 8), 0)
        scan(sub(ee, 8, NE + 8), ecrow, ecrow, ALU.add, ALU.max)
        pe = pick16(sub(ee, 8, NE + 8))
        eel = ti(pe, s16, ALU.mult)
        big = ti(ec, 4096.0, ALU.mult)
        offu = u16(tti(tti(cy, big, ALU.subtract), tti(eel, ec, ALU.subtract), ALU.max))
        vrow = tt(rows(NE), IND(t256, slu), jrow if last else ndrow, ALU.add)
        vw = gfill(rows(C + NE), 2048)
        cp(IND(vw, offu), vrow)
        keep = rows(C)
        either(lambda keep=keep, vw=vw: ts(keep, sub(vw, 0, C), 2048.0, ALU.is_equal),
               lambda keep=keep, vw=vw: act(keep, sub(vw, 0, C), ACT.Relu, bias=2049.0, scale=-1.0))
        hv = ti(pick16(scan(rows(C), keep, sub(vw, 0, C), ALU.mult, ALU.add)), s16, ALU.mult)
        fu = u16(ti(hv, 8, ALU.arith_shift_right))
        code = ti(hv, 255, ALU.bitwise_and)
        codeu = u16(code)
        cp(IND(early, slu), as_row(u16(mp), DB[t - 1] + KX) if t else jrow)
        mpn = tti(tti(ti(pe, s16, ALU.mult, float(XB[t + 1] - 1), ALU.add), big, ALU.min), mp, ALU.max)
        mrow = as_row(u16(mpn), XB[t + 1] + C)
        nb = NE if last else KX
        bu = list4(aff(rows(nb), IND(mrow, sub(yu, 0, nb // 16))))

        pool[0], used["rs"] = "rs", 0
        xq, xs = W("xq", C * t, C * t + C), W("xs", C * t, C * t + C)
        quant(xq, xs, xt[t])
        sv = mm(1, up, ups, xq, xs)
        ss = mm(0, up, ups, xq, xs)
        neg, ng = rows(C), rows(C)
        for a, b in ((224, C), (0, 224)):
            scan(sub(neg, a, b), sub(k16, a, b), tt(sub(ng, a, b), sub(sv, a, b), sub(dm, a, b), ALU.mult), ALU.mult, ALU.add)
        ga = new("lf", 20)
        gfill(sub(ga, 0, 1), 0)
        pc = W("ps", 512 * 6, 512 * 6 + C)
        for q_, (a, n_) in enumerate(TILES):
            for k in range(4):
                m = 20 - 4 * q_ - k
                if m == 20:
                    act(W("sg", 4 * a, 4 * (a + C), 4), tt(rows(C), sv, aff(rows(C), IND(neg, m15u)), ALU.add), ACT.Sign)
                else:
                    act(W("sg", 4 * a + k, 4 * (a + 16 * m), 4), sub(ss, 0, 16 * m), ACT.Sign, bias=sub(neg, 16 * m + 15, 16 * m + 16), acc=sub(ga, m, m + 1))
            sq, sp = W("sq", a, a + n_), W("sp", a, a + n_)
            quant(sq, sp, W("sg", 4 * a, 4 * (a + n_)))
            mm(6, bdq, bds, sq, sp, q_ == 0, q_ == len(TILES) - 1)
        key = tt(rows(C), pc, tt(rows(C), IND(t320, u16(ga, float(C), ALU.add)), base, ALU.add), ALU.add)
        kl = ttf(tf(pick16(pc), s16, ALU.mult, WHOLE, ALU.add), ttf(tf(ga, float(C), ALU.mult), bl, ALU.add), ALU.add)
        mv = MV2[t]
        m0 = 20 - mv
        pu = new("lu", 20)
        cp(sub(pu, 0, m0), ttf(count_below(key, sub(kl, 0, m0)), sub(pad, 0, m0), ALU.add))
        if mv:
            for m in range(mv):
                ts(W("cc", C * m, C * m + C), key, sub(kl, m0 + m, m0 + m + 1), ALU.is_lt, 2.0, ALU.mult)
            scan(W("cs", 0, mv * C), sub(kp2, 0, mv * C), W("cc", 0, mv * C), ALU.mult, ALU.add)
            both = ttf(W("cs", C // 2 - 1, mv * C, C), W("cs", C - 1, mv * C, C), ALU.add)
            ts(sub(pu, m0, 20), ttf(both, sub(pad, m0, 20), ALU.add), float(1 - C), ALU.add)
        cp(IND(tbl, pu), sub(io, XB[t], XB[t] + C))
        zu = list4(aff(rows(C), IND(early, pu)))
        su = list4(aff(rows(C), IND(tbl, fu)), bx[t])
        top = XB[t] + C if t == 0 else DB[t - 1] + KX
        zt = W("zt", 4 * C * t, 4 * C * (t + 1))
        zq, zs = W("zq", C * t, C * t + C), W("zs", C * t, C * t + C)
        f = 0.5 if last else 1.0
        for h, (a, e_) in enumerate(((0, ZA), (ZA, C))):
            tt(sub(zt, 4 * a, 4 * e_), IND(W("st", 0, 4 * top), sub(zu, a // 4, e_ // 4)), W("xh", 4 * a, 4 * e_), ALU.add)
            quant(sub(zq, a, e_), sub(zs, a, e_), sub(zt, 4 * a, 4 * e_))
            for b in range(4):
                pr = mm((2 + 4 * h + b) % 8, W("wq", 128 * b, 128 * b + 128), W("wp", 128 * b, 128 * b + 128), sub(zq, a, e_), sub(zs, a, e_))
                relu(W("rr", 4 * a + b, 4 * e_, 4), pr, 0.03125 * f)
        for a, e_ in PIECES:
            zg = aff(W("zg", 16 * a, 16 * e_), IND(zt, sub(su, a, e_)), f)
            xh = W("st", 4 * XB[t + 1] + 16 * a, 4 * XB[t + 1] + 16 * e_)
            tt(xh if last else sub(xt[t + 1], 16 * a, 16 * e_), IND(W("rr", 0, 4 * C), sub(su, a, e_)), zg, ALU.add)
            if not last:
                halve(t + 1, 16 * a, 16 * e_)
        pool[0] = "rw"
        win = W("st", 0, 4 * (XB[t + 1] + C))
        bt, bq, bs = W("bt", 128 + 4 * KX * t, 128 + 4 * KX * (t + 1)), W("bq%d" % t, 0, 128), W("bs%d" % t, 0, 128)
        if last:
            aff(sub(bt, 0, 2 * KX), IND(win, sub(bu, 0, 12)), 2.0)
            aff(sub(bt, 2 * KX, 4 * KX), IND(win, sub(bu, 12, 24)), 2.0)
        else:
            aff(bt, IND(win, sub(bu, 0, 24)), 2.0)
        quant(bq, bs, sub(bt, -128, 4 * KX))
        lq, ls = W("lq", 128 + KX * t, 128 + KX * (t + 1)), W("ls", 128 + KX * t, 128 + KX * (t + 1))
        rid, pid, _ = topo.addr(partner[t])
        mask = topo.mask(core, partner[t])
        ne = len(topo.engines(core, partner[t]))

        def send(src, dst, cast, t=t, rid=rid, pid=pid, mask=mask):
            return lambda q: q.remote_dma(ap(dst, cast), ap(src, cast), T.sem["arr%d" % t], T.sem["snt%d" % t], pid, rid, mask)
        i1 = add("g", send(sub(bq, 32, 128), lq, dt.uint8), [bq], [], 0.3, 0.0, "r")
        i2 = add("g", send(sub(bs, 32, 128), ls, None), [bs], [], 0.3, 0.0, "r")
        ia = add("x", None, [bq, bs], [lq, ls], 0.0, 2.0 if last else 6.0, "a")
        ops[ia]["after"], ops[ia]["sem"], ops[ia]["n"] = [i1, i2], "arr%d" % t, 2 * ne
        for b in range(4):
            pd = mm(2 + b, W("eq", 128 * b, 128 * b + 128), W("es", 128 * b, 128 * b + 128), sub(lq, -32, KX), sub(ls, -32, KX))
            if last:
                aff(W("mt", b, 4 * KX, 4), sub(pd, 32, 128))
            else:
                aff(W("st", 4 * DB[t] + b, 4 * DB[t] + 4 * KX, 4), sub(pd, 32, 128), 0.5)
        if not last:
            mp = tti(ti(jm, float(DB[t]), ALU.add), mpn, ALU.max)
            base, bl, pad = node_keys(code, codeu)
            tab, la, lb, uc, fo = ee, l1u, l2u, un, fn_

    otb = aff(W("otb", 0, C), IND(sub(io, 0, NE), codeu))
    for gi in range(8):
        dma("y", lambda q, gi=gi: q.dma_start(T.ot[gi:gi + 1, :], T.otb[16 * gi:16 * gi + 1, :]), [otb], [], 8.0)
    xq, xs = W("xq", 3 * C, 4 * C), W("xs", 3 * C, 4 * C)
    quant(xq, xs, aff(xt[3], W("st", 4 * XB[3], 4 * NS), 2.0))
    yb = aff(W("yb", 0, C), mm(0, W("vq", 0, 128), W("vs", 0, 128), xq, xs))
    dma("y", lambda q: q.dma_start(T.y[:], T.yb[:]), [yb], [], 2.6)
    aff(W("mt", 4 * KX, 4 * NE), IND(win, sub(bu, 24, 64)), 2.0)
    for a, queues, lat in ((128, "yyyyy", 3.0), (0, "ysysy", 1.8)):
        mq, ms = W("mq", a, a + 128), W("ms", a, a + 128)
        quant(mq, ms, W("mt", 4 * a, 4 * a + 512))
        dma(queues[0], lambda q, a=a, mq=mq: q.dma_start(T.oc[:, 4 * a:4 * a + 512], ap(mq, dt.uint8)), [mq], [], lat + 0.2)
        for k in range(4):
            dma(queues[1 + k], lambda q, a=a, k=k: q.dma_start(T.osc[4 * k:4 * k + 4, a:a + 128], T.ms[32 * k:32 * k + 4, a:a + 128]), [ms], [], lat)
    return ops


def order(ops, others=()):
    n = len(ops)
    seen = {}
    for i, o in enumerate(ops):
        dep = set(o.get("after", []))
        for w in o["rd"]:
            for j, x, wr in seen.get(w[0], []):
                if (wr or (w[0] == "ps" and (ops[j]["eng"] != o["eng"] or "alt" in o or "alt" in ops[j]))) and meets(w, x):
                    dep.add(j)
        for w in o["wr"]:
            for j, x, wr in seen.get(w[0], []):
                if meets(w, x):
                    dep.add(j)
        dep.discard(i)
        o["dep"] = dep
        for w in o["rd"]:
            seen.setdefault(w[0], []).append((i, w, False))
        for w in o["wr"]:
            seen.setdefault(w[0], []).append((i, w, True))
    nxt = [[] for _ in range(n)]
    for i, o in enumerate(ops):
        for j in o["dep"]:
            nxt[j].append(i)
    prv = [sorted(o["dep"]) for o in ops]
    lat = [o["lat"] for o in ops]
    wait = PLANS[0][5]

    def run(before, after, pr, en, back):
        cost = [o["alt"][en[i]][1] if "alt" in o else o["cost"] for i, o in enumerate(ops)]
        left = [len(x) for x in before]
        ready = {e: {} for e in "vspgyx"}
        for i in range(n):
            if left[i] == 0:
                ready[en[i]][i] = lat[i] if back else 0.0
        free, seq, t0, t1 = {e: 0.0 for e in ready}, [], [0.0] * n, [0.0] * n
        for _ in range(n):
            a, _p, e, i = min((max(r, free[e]), -pr[i], e, i) for e in ready for i, r in ready[e].items())
            lim = a + LOOK * cost[i]
            for j, r in ready[e].items():
                if pr[j] > pr[i] and r < lim:
                    i = j
            a = max(ready[e].pop(i), free[e])
            t0[i], free[e] = a, a + cost[i]
            t1[i] = free[e] + (0.0 if back else lat[i])
            seq.append(i)
            for j in after[i]:
                left[j] -= 1
                if left[j] == 0:
                    ready[en[j]][j] = max(t1[k] for k in before[j]) + wait + (lat[j] if back else 0.0)
        return seq, t0, t1

    if not KEPT:
        pr = [0.0] * n
        for i in range(n - 1, -1, -1):
            pr[i] = ops[i]["cost"] + lat[i] + wait + max([pr[j] for j in nxt[i]] + [0.0])
        free_ = [i for i in range(n) if "alt" in ops[i]]
        en = ["s" if "alt" in o else o["eng"] for o in ops]
        best, now, seed = None, None, [SEED]

        def rnd():
            seed[0] = (seed[0] * 1103515245 + 12345) % 2147483648
            return seed[0] / 2147483648.0
        for turn in range(TURNS):
            if now is not None:
                pr, en = list(now[5]), list(now[4])
                move = rnd()
                if move < 0.3:
                    i = free_[int(rnd() * len(free_))]
                    en[i] = "v" if en[i] == "s" else "s"
                elif move < 0.93:
                    a = int(rnd() * n)
                    d = NOISE * (rnd() - 0.5) * rnd()
                    for i in range(a, min(n, a + 1 + int(rnd() * rnd() * 40))):
                        pr[i] += d
                else:
                    pr = run(nxt, prv, now[3], en, True)[2]
            seq, t0, t1 = run(prv, nxt, pr, en, False)
            mark = max(t1) + SOON * sum(t1) / n
            for k, other in enumerate(others):
                wake, free, end = PLANS[k + 1][5], {e: 0.0 for e in "vspgyx"}, [0.0] * n
                for i in seq:
                    a = free[en[i]]
                    for j in prv[i]:
                        if end[j] > a:
                            a = end[j]
                    o = other[i]
                    free[en[i]] = a = a + (o["alt"][en[i]][1] if "alt" in o else o["cost"])
                    end[i] = a + lat[i] + wake
                mark += max(end)
            if now is None or mark <= now[0] + HEAT * (1.0 - turn / TURNS) * rnd():
                now = (mark, seq, t0, t1, en, pr)
                if best is None or mark < best[0]:
                    best = now
        KEPT.append(best)
    best = KEPT[0]
    for i, o in enumerate(ops):
        if "alt" in o:
            o["eng"] = best[4][i]
            o["fn"], o["cost"] = o["alt"][o["eng"]]
        o["t0"], o["t1"] = best[2][i], best[3][i]
    return best[1]


def rank_program(g, core, T, topo):
    rank = T.rank_of(core)
    if rank is None:
        return
    ops = plan(T, topo, core, rank)
    seq = order(ops, [] if KEPT else [plan(T, topo, core, rank, k) for k in range(1, len(PLANS))])
    queue = {"v": g.vector, "s": g.scalar, "p": g.tensor, "g": g, "y": g.sync}
    counter = {"v": "cv", "s": "cs", "p": "cp", "g": "cg"}
    count = {s: 0 for s in SEMAPHORES}
    known = {e: {} for e in queue}
    nd = 0
    for i in seq:
        o = ops[i]
        if o["kind"] == "a":
            o["mark"], o["clock"] = (o["sem"], o["n"]), {o["sem"]: o["n"]}
            count[o["sem"]] = o["n"]
            count["snt" + o["sem"][3:]] = o["n"]
            continue
        q, kn = queue[o["eng"]], known[o["eng"]]
        for j in sorted(o["dep"], key=lambda j: -ops[j]["t1"]):
            if ops[j]["kind"] == "r":
                continue
            s, c = ops[j]["mark"]
            if kn.get(s, 0) < c:
                q.wait_ge(T.sem[s], c)
                for s2, c2 in ops[j]["clock"].items():
                    kn[s2] = max(kn.get(s2, 0), c2)
        ins = o["fn"](q)
        if o["kind"] == "r":
            continue
        if o["kind"] == "d":
            s, inc = "d%d" % nd, 16
            nd += 1
        else:
            s, inc = counter[o["eng"]], 1
        ins.then_inc(T.sem[s], inc)
        count[s] += inc
        o["mark"] = (s, count[s])
        o["clock"] = dict(kn)
        o["clock"][s] = count[s]
    for s in SEMAPHORES:
        if count[s]:
            g.wait_ge(T.sem[s], count[s])
